import numpy as np, ml_dtypes
CORES = [1,5,17,21,33,37,49,53]
N = 8
BF = ml_dtypes.bfloat16
W, H0, L, RO, Q = 4096, 1536, 192, 3, 2
def base(rng):
    price = rng.integers(0, 101, (N, 8, 1, W)) + rng.integers(0, 28, (N, 8, 16, W))
    packs = rng.integers(0, W, (N, 8, 16, H0)); prev = rng.integers(0, H0, (N, 8, H0)); lots = rng.integers(0, W, (N, 8, 16, L))
    lots[:, :, 0, ::4] = lots[:1, :, 0, ::4]
    o = np.stack([rng.permutation(np.array([5, 20, 35, 50, 60, 70, 80, 90])) for q in range(N)])
    slack = o[:, :, None, None] + rng.integers(0, 9, (N, 8, 16, RO))
    return price, packs, prev, lots, rng.integers(1, 8, (N, 8, 16)), rng.integers(0, 16, (N, 8, 16)), slack
def pack(price, packs, prev, lots, inc, wt, slack):
    c = lambda a, n: np.ascontiguousarray(np.reshape(a, (N, 128, n))).astype(np.int32)
    return {"price": np.ascontiguousarray(price.reshape(N, 128, W)).astype(np.float32).astype(BF), "packs": c(packs, H0), "prev": np.ascontiguousarray(prev).astype(np.int32),
            "lots": c(lots, L), "inc": c(inc, 1), "wt": c(wt, 1), "slack": c(slack, RO)}
def edge(rng, hi, *s):
    return np.where(rng.random(s) < 0.2, rng.integers(0, hi + 1, s), hi * rng.integers(0, 2, s))
def setup_inputs(rng):
    return pack(*base(rng))
def setup_inputs_spread(rng):
    price, packs, prev, lots, inc, wt, slack = base(rng)
    price = np.minimum((np.exp2(7.65 * rng.random((N, 8, 1, W))) * rng.random((N, 8, 16, W))).astype(np.int64), 200)
    packs = np.minimum((W * rng.random((N, 8, 16, H0)) ** 3).astype(np.int64), W - 1)
    lots = W - 1 - np.minimum((W * rng.random((N, 8, 16, L)) ** 2).astype(np.int64), W - 1)
    prev = np.minimum((H0 * rng.random((N, 8, H0)) ** 2).astype(np.int64), H0 - 1)
    slack = np.minimum(np.exp2(8 * rng.random((N, 8, 1, 1)) * rng.random((N, 8, 16, RO))).astype(np.int64) - 1, 255)
    return pack(price, packs, prev, lots, inc, wt, slack)
def setup_inputs_ends(rng):
    hi = np.where(np.arange(8) == 6, 127, 200)[None, :, None, None]
    k = rng.integers(0, 3, (N, 8, 1, W)); price = hi * np.where(k == 2, rng.integers(0, 2, (N, 8, 16, W)), k)
    price[..., 0] = 0; price[..., W - 1] = hi[..., 0]
    price[:, 2:4, :, 0] = 200; price[:, 2:4, :, W - 1] = 0; price[:, 5, 9:, W - 1] = 0
    packs = edge(rng, W - 1, N, 8, 16, H0); prev = edge(rng, H0 - 1, N, 8, H0); lots = edge(rng, W - 1, N, 8, 16, L)
    inc = 1 + 6 * rng.integers(0, 2, (N, 8, 16)); inc[:, 7] = 7; inc[:, 6, 0] = 1
    o = np.argsort(rng.random((N, 8, 16)), axis=2)
    slack = np.repeat((255 * (o >= np.array([16, 9, 16, 9, 12, 16, 8, 8])[None, :, None]))[..., None], RO, axis=3)
    wt = 15 * rng.integers(0, 2, (N, 8, 16)); wt[:, 7] = 0
    full = np.array([15] * 8 + [9] + [0] * 7); wt[:, 6] = full[o[:, 6]]; wt[:, 0] = full[o[:, 0]]
    c = np.array([0, 3, L - 1]); lots[:, 6, 0, c] = W - 1; lots[:, 6, 15, c] = W - 1
    v = np.arange(W)
    back = lambda t, to: int(np.argmax(((v + (v >> 5) + 77 * (t + 1)) & (W - 1)) == to))
    lots[:, 7, 0, c] = W - 1; lots[:, 7, 1, c] = back(0, W - 1); lots[:, 7, 2, c] = back(0, back(1, W - 1))
    return pack(price, packs, prev, lots, inc, wt, slack)
def setup_inputs_corners(rng):
    price, packs, prev, lots, inc, wt, slack = base(rng); a = np.arange(H0)
    kinds = [a, np.maximum(a - 1, 0), 0 * a, 0 * a + H0 - 1, (a + 1) % H0, a ^ 1, H0 - L + a % L]
    for q in range(N):
        for g, k in enumerate(rng.permutation(8)):
            if k < 7: prev[q, g] = kinds[int(k)]
            wt[q, g] = (0, 15, 1, 7)[int(rng.integers(0, 4))] if k < 4 else wt[q, g]
            inc[q, g] = 1 if k % 3 == 0 else 7 if k % 3 == 1 else inc[q, g]
    s = [int(g) for g in rng.permutation(8)]
    for g in s[:4]: slack[:, g] = 255
    lots[:, s[0], :RO] = W - 1; wt[:, s[0]] = 0; price[:, s[0], :, W - 1] = 127; inc[:, s[0]] = 7
    lots[:, s[1], 0] = 0; price[:, s[1], :, 0] = 127 * rng.integers(0, 2, (N, 16))
    m = rng.permutation(W); lots[:, s[2], 0] = m[(np.arange(N * L) % (W - 1) + 1).reshape(N, L)]; lots[int(rng.integers(0, N)), s[2], 0, L - 1] = m[0]
    for q in range(N): lots[q, s[3], 0] = rng.permutation(W)[:L]
    packs[:, s[4], :, H0 - L:] = lots[:, s[4]]
    slack[:, s[4]] = 0; slack[:, s[5]] = 0; h = W // 2
    price[:, s[5], :, :h] = rng.integers(0, 3, (N, 16, h)); price[:, s[5], :, h:] = 127; lots[:, s[5]] = rng.integers(h, W, (N, 16, L)); packs[:, s[5]] = rng.integers(0, h, (N, 16, H0))
    nxt = lambda z, u, t: (((z * (2 * u + 1)) >> 5) + z + 77 * (t + 1)) & (W - 1)
    g = s[6]; b = int(rng.integers(0, N)); k = L // 2
    wt[:, g] = 0; inc[:, g] = 7; inc[b, g] = 1 + rng.permutation(16) % 5
    slack[:, g] = 255; slack[:, g, :, RO - 1] = 254 - rng.integers(0, 55, (N, 16)) * (np.arange(N) % 2)[:, None]
    e = rng.integers(0, W, L); own = nxt(e, 0, 0); own[k:] = nxt(own[k:], 0, 1)
    lots[:, g, 0] = own; lots[:, g, 1, :k] = e[:k]; lots[:, g, 2, k:] = e[k:]
    dear = np.zeros(W, bool); dear[own] = True; low = rng.random(W) < 0.5
    v = 200 - (rng.random((N, 16, W)) * np.where(low, 32, 8)).astype(np.int64)
    v[b] = np.where(low, rng.integers(0, 4, (16, W)), v[b])
    price[:, g] = np.where(dear, v, rng.integers(0, 3, W))
    g = s[7]; wt[:, g] = 15; inc[:, g] = 7; slack[:, g] = 255; price[:, g] = 200
    e = rng.integers(0, W, L); lots[:, g, 1] = e; lots[:, g, 0] = nxt(e, (16 * 15 * 200) & 1023, 0)
    return pack(price, packs, prev, lots, inc, wt, slack)
def setup_inputs_ties(rng):
    price, packs, prev, lots, inc, wt, slack = base(rng)
    s0 = rng.integers(0, 21, (N, 8, 16)); b = rng.integers(0, 106, (N, 8, 16)); slack = np.repeat(s0[..., None], RO, axis=3)
    n = rng.choice(np.array([0, 7, 8, 9, 10, 16]), (N, 8, 1, W)); low = rng.random((N, 8, 1, W)) < 0.5
    o = np.argsort(rng.random((N, 8, W, 16)), axis=3).transpose(0, 1, 3, 2)
    price = b[..., None] + np.where(low, 0, s0[..., None] + (o < n))
    return pack(price, packs, prev, lots, inc, wt, slack)
def check_inputs(d):
    bad = []
    for k, lo, hi in (("price", 0, 200), ("packs", 0, W - 1), ("prev", 0, H0 - 1), ("lots", 0, W - 1), ("inc", 1, 7), ("wt", 0, 15), ("slack", 0, 255)):
        v = np.asarray(d[k]).astype(np.float64)
        if not (np.min(v) >= lo and np.max(v) <= hi): bad.append("range of " + k)
        elif np.any(v != np.floor(v)): bad.append("whole numbers in " + k)
    return bad
def pick(p, t):
    return np.take_along_axis(p, t.reshape(N, 8, 1, 16 * L), 3).reshape(N, 8, 16, 16, L)
def reference(price, packs, prev, lots, inc, wt, slack):
    p = price.astype(np.float32).astype(np.int64).reshape(N, 8, 16, W)
    h = np.zeros((N, 8, 16, H0 + RO * L), np.int64); h[..., :H0] = packs.reshape(N, 8, 16, H0)
    v = np.zeros((N, 8, H0 + RO * L), np.int64); v[..., :H0] = prev
    t = lots.astype(np.int64).reshape(N, 8, 16, L)
    up = inc.astype(np.int64).reshape(N, 8, 16, 1); wr = wt.astype(np.int64).reshape(N, 8, 16, 1); sl = slack.astype(np.int64).reshape(N, 8, 16, RO)
    a = np.zeros((N, 8, L), np.int64) + (H0 - L + np.arange(L))
    for rnd in range(RO):
        x = pick(p, t); bind = np.zeros((N, 8, L), np.int64) - 1
        for e in range(Q):
            anc = np.take_along_axis(h, a[:, :, None, :], 3); y = pick(p, anc)
            rows = np.add.reduce((x - y > sl[:, :, :, rnd][:, :, :, None, None]).astype(np.int64), axis=2)
            rev = rows >= 9
            t = np.where(rev, anc, t); x = np.where(rev[:, :, None], y, x)
            bind = np.where(np.any(rev, axis=2), a, bind); last = a
            a = np.take_along_axis(v, a, 2)
        lo = H0 + L * rnd
        h[..., lo:lo + L] = t; v[..., lo:lo + L] = np.where(bind >= 0, bind, last)
        flag = np.zeros((N, 8, W), np.int64); np.put_along_axis(flag, t[:, :, rnd], 1, 2)
        offer = p * flag[:, :, None]; s = np.add.reduce(offer, axis=0)[None] - offer
        if rnd + 1 < RO:
            u = np.add.reduce(wr * np.max(x, axis=3), axis=2) & 1023
            t = (((t * (2 * u + 1)[:, :, None]) >> 5) + t + 77 * (rnd + 1)) & (W - 1)
            a = np.zeros((N, 8, L), np.int64) + (lo + np.arange(L))
        p = np.minimum(p + ((up * s) >> 6), 255)
    return {"yp": p.reshape(N, 128, W).astype(np.float32).astype(BF), "yh": np.ascontiguousarray(h[..., H0:]).reshape(N, 128, RO * L).astype(np.float32), "yv": np.ascontiguousarray(v[..., H0:]).astype(np.float32)}

@@ -1,0 +1,555 @@
+import numpy as np
+from concourse.bass import DstId, RemoteDMATransfer
+from concourse.mybir import dt, AluOpType, AxisListType, ActivationFunctionType
+
+A = AluOpType
+AF = ActivationFunctionType
+MAGIC = 12582912.0
+NL = 192
+E = 16 * NL
+W = 4096
+WW = W + 16
+CUTS = [0, 64, 128, 192]
+BLOCKS = [0, 1024, 2048, 3072, 3584, W]
+NB = len(BLOCKS) - 1
+SCRATCH = {}
+for _d, _n, _names in (
+        ("bfloat16", W, "ph c pf"), ("bfloat16", WW, "w0 w1 w2 pl"), ("float32", W, "dd"), ("int32", 1536, "pk"),
+        ("int32", NL, "lt pnr ui uj pr ps sm tn"), ("int32", 12, "pvi"), ("uint16", 24, "pvo of"), ("uint16", 12, "vl"),
+        ("int32", 8, "cs cso pci"), ("float32", 8, "csf nsl cof pcf"), ("float32", 128, "cd"), ("float32", 384, "ts par12 at tt q0 q1 q2"),
+        ("bfloat16", 128, "bo nb eq idm nid qk dg qm wth wto cstb cst2"), ("bfloat16", 512, "oneb"), ("bfloat16", 2048, "sel16"),
+        ("bfloat16", E, "rm ind x2 sc"), ("float32", E, "xs0 xs1"), ("bfloat16", NL, "cse v0"), ("bfloat16", 384, "mk0 mk1"),
+        ("float32", NL, "cm dm pb0 pb1 pb2 a1f sel tf o2f par0 b1f tc cmk cs1 cs2"),
+        ("uint16", NL, "tu0 a0u a1u t1u t2u0 t2u1 t2u2 o2u b1u tnu"), ("float32", 12, "ct1 ct2"),
+        ("uint16", 576, "m4u mo"), ("float32", 384, "mof")):
+    for _k in _names.split():
+        SCRATCH[_k] = ("sbuf", [128, _n], _d)
+MSG = []
+for _k, _n, _d in [("cst", 1, "int32"), ("pri", 512, "bfloat16"), ("t2", 24, "uint16"), ("m4", 72, "uint16"), ("y1", 24, "float32"),
+                   ("y2", 24, "float32"), ("par", 3, "float32")] + [("o%d" % _b, (BLOCKS[_b + 1] - BLOCKS[_b]) // 8, "bfloat16") for _b in range(NB)]:
+    MSG.append(_k)
+    SCRATCH["s_" + _k] = SCRATCH["l_" + _k] = ("dram", [8, 128, _n], _d)
+BANKS = ["cn0", "cn1", "vs", "db0", "db1", "db2", "db3", "db4"]
+for _k in BANKS:
+    SCRATCH[_k] = ("psum", [128, 512], "float32")
+SEMAPHORES = ["vv", "ss", "pe", "gg", "lsem"] + ["d%d" % _i for _i in range(64)] + ["ar_" + _m for _m in MSG]
+
+
+def rank_program(g, core, T, topo):
+    rank = T.rank_of(core)
+    if rank is None:
+        return
+    cores = [int(c) for c in T.cores]
+    N = len(cores)
+
+    eng = {"v": g.vector, "s": g.scalar, "p": g.tensor, "g": g, "y": g.sync}
+    sem_of = {"v": "vv", "s": "ss", "p": "pe", "g": "gg"}
+    count = {"vv": 0, "ss": 0, "pe": 0, "gg": 0, "d": 0}
+    know = {q: {} for q in eng}
+    snap = {}
+    hist = {}
+    total = {}
+    seen = {}
+
+    def wait(q, sem, val):
+        if know[q].get(sem, 0) >= val:
+            return
+        eng[q].wait_ge(T.sem[sem], val)
+        seen[sem] = max(seen.get(sem, 0), val)
+        know[q][sem] = val
+        for k, n in snap.get((sem, val), {}).items():
+            know[q][k] = max(know[q].get(k, 0), n)
+
+    def settle(q, reads, writes, is_dma):
+        for (b, lo, hi), wr in [(r, False) for r in reads] + [(w, True) for w in writes]:
+            bank = b in BANKS
+            for e in hist.get(b, []):
+                over = e[0] < hi and lo < e[1]
+                if e[2] == q and not is_dma:
+                    need = over and (e[5] or (wr and bank))
+                else:
+                    need = bank or (over and (wr or e[5]))
+                if need:
+                    wait(q, e[3], e[4])
+
+    def record(q, sem, val, reads, writes):
+        for (b, lo, hi) in writes:
+            hist[b] = [e for e in hist.get(b, []) if not (lo <= e[0] and e[1] <= hi)] + [(lo, hi, q, sem, val, True)]
+        for (b, lo, hi) in reads:
+            old = hist.get(b, [])
+            hist[b] = [e for e in old if not (e[:3] == (lo, hi, q) and not e[5] and q != "d")] + [(lo, hi, q, sem, val, False)]
+
+    def run(q, reads, writes, *fns):
+        settle(q, reads, writes, False)
+        for f in fns[:-1]:
+            f()
+        sem = sem_of[q]
+        count[sem] += 1
+        val = total[sem] = count[sem]
+        fns[-1]().then_inc(T.sem[sem], 1)
+        snap[(sem, val)] = dict(know[q])
+        snap[(sem, val)][sem] = val
+        record(q, sem, val, reads, writes)
+
+    def dma(q, out, in_, reads, writes):
+        settle(q, reads, writes, True)
+        sem = "d%d" % count["d"]
+        count["d"] += 1
+        total[sem] = 16
+        eng[q].dma_start(out, in_).then_inc(T.sem[sem], 16)
+        snap[(sem, 16)] = dict(know[q])
+        record("d", sem, 16, reads, writes)
+
+    def full(name):
+        return (name, 0, 1 << 20)
+
+    def col(x, lo=0, hi=NL):
+        if x in SCRATCH:
+            x = (x, 0)
+        b, st = x[0], x[2] if len(x) > 2 else 1
+        i, j = x[1] + lo * st, x[1] + (hi - 1) * st + 1
+        return (T[b][:, i:j] if st == 1 else T[b][:, i:j:st]), (b, i, j)
+
+    def V(reads, writes, f):
+        run("v", reads, writes, f)
+
+    def S(reads, writes, f):
+        run("s", reads, writes, f)
+
+    v, s, te = g.vector, g.scalar, g.tensor
+
+    def vt(out, in0, in1, op):
+        return lambda: v.tensor_tensor(out, in0, in1, op)
+
+    def vc(out, in_):
+        return lambda: v.tensor_copy(out, in_)
+
+    def v1(out, in0, s1, op):
+        return lambda: v.tensor_scalar(out, in0, s1, None, op)
+
+    def v2(out, in0, s1, s2, op0, op1):
+        return lambda: v.tensor_scalar(out, in0, s1, s2, op0, op1)
+
+    def copy(out, in_):
+        V([in_[1]], [out[1]], vc(out[0], in_[0]))
+
+    def fill(b, lo, hi, x):
+        V([], [(b, lo, hi)], lambda: v.memset(T[b][:, lo:hi], x))
+
+    def weave(*chains):
+        for i in range(max(len(c) for c in chains)):
+            for c in chains:
+                if i < len(c):
+                    c[i]()
+
+    def nothing():
+        pass
+
+    others = [(rank + j) % N for j in range(1, N)]
+    away = [d for d in others if topo.chip(cores[d]) != topo.chip(core)]
+    near = [d for d in others if topo.chip(cores[d]) == topo.chip(core)]
+    offe = topo.engines(core, cores[away[0]])
+    one = [e for e in topo.engines(core, cores[near[0]]) if e not in offe]
+    turn = [0]
+    arrive = {m: 0 for m in MSG}
+
+    def fused(m, plan):
+        settle("g", [full("s_" + m)], [], True)
+        tr = []
+        for d, es in plan:
+            rid, pid, _e = topo.addr(cores[d])
+            tr.append(RemoteDMATransfer(dst_ids=[DstId(rid=rid, pnc=pid)], dma_engine_mask=sum(1 << e for e in es),
+                                        remote_sem=T.sem["ar_" + m], src=T["s_" + m][d], dst=T["l_" + m][rank]))
+        g.remote_dma_fused(tr, local_sem=T.sem.lsem)
+        n = sum(len(es) for d, es in plan)
+        total["lsem"] = total.get("lsem", 0) + n
+        arrive[m] += n
+
+    def send(m):
+        plan = [(d, [offe[(turn[0] + j) % len(offe)]]) for j, d in enumerate(away)]
+        turn[0] += len(away)
+        fused(m, plan + [(d, one[0:3:2]) for d in near])
+
+    def send_wide(m):
+        fused(m, [(d, offe[2 * j:2 * j + 2]) for j, d in enumerate(away[:4])] + [(d, one[0:3:2]) for d in near])
+        fused(m, [(d, offe[4 * j:4 * j + 4]) for j, d in enumerate(away[4:])])
+
+    def landed(q, m):
+        total["ar_" + m] = arrive[m]
+        wait(q, "ar_" + m, arrive[m])
+
+    mine = slice(16 * rank, 16 * rank + 16)
+
+    def stage(m, in_, reads, rows=None):
+        dma("y", T["s_" + m][:], in_[:] if rows is None else in_[0:128:16, :], reads, [full("s_" + m)])
+        dma("y", T["l_" + m][rank], in_[mine, :] if rows is None else in_[16 * rank:16 * rank + 1, :], reads, [full("l_" + m)])
+
+    def take(q, m, out, writes):
+        landed(q, m)
+        dma(q, out, T["l_" + m][:], [full("l_" + m)], writes)
+
+    fill("cs", 0, 8, 0)
+    fill("pnr", 0, NL, 0)
+    fill("mk0", 0, 384, 0.0)
+    fill("mk1", 0, 384, 0.0)
+    dma("s", T.lt[:], T.lots[:], [], [full("lt")])
+    dma("y", T.cs[:, 0:3], T.slack[:], [], [("cs", 0, 3)])
+    dma("y", T.ph[:], T.price[:], [], [full("ph")])
+    dma("s", T.pk[:, 1344:1536], T.packs[:, 1344:1536], [], [("pk", 1344, 1536)])
+    dma("s", T.pvi[:], T.prev[:, 1344:1536], [], [full("pvi")])
+    dma("y", T.pk[:, 0:1344], T.packs[:, 0:1344], [], [("pk", 0, 1344)])
+    dma("s", T.cs[:, 3:4], T.inc[:], [], [("cs", 3, 4)])
+    dma("s", T.cs[:, 4:5], T.wt[:], [], [("cs", 4, 5)])
+    dma("s", T.pnr[0:128:16, :], T.prev[:, 1344:1536], [], [full("pnr")])
+    stage("pri", T.price, [])
+    stage("cst", T.cs, [full("cs")])
+
+    def iota(b, lo, hi, pat, base, cm, **kw):
+        run("g", [], [(b, lo, hi)], lambda: g.iota(T[b][:, lo:hi], pat, base, cm, **kw))
+    small = {"allow_small_or_imprecise_dtypes": True}
+    iota("pci", 0, 1, [[0, 1]], 0, 1)
+    iota("cd", 0, 128, [[1, 8], [0, 16]], 0, 0, **small)
+    iota("cm", 0, NL, [[0, 12], [1, 16]], 0, 0, **small)
+    for t in range(3):
+        iota("pb%d" % t, 0, NL, [[1, NL]], 1344 + NL * t, 0, **small)
+    iota("w0", 0, WW, [[0, WW]], 0, 0, **small)
+    V([("pci", 0, 1)], [("pci", 1, 2)], v1(T.pci[:, 1:2], T.pci[:, 0:1], 15, A.bitwise_and))
+    V([("pci", 0, 1)], [("pci", 2, 3)], v1(T.pci[:, 2:3], T.pci[:, 0:1], 4, A.logical_shift_right))
+    fill("sel16", 0, 2048, 0.0)
+    V([("pci", 1, 3)], [("pcf", 1, 3)], vc(T.pcf[:, 1:3], T.pci[:, 1:3]))
+    copy(col("tu0"), col("lt"))
+    copy(col("csf", 0, 3), col("cs", 0, 3))
+    V([full("cd"), ("pcf", 2, 3)], [full("bo")], v1(T.bo[:], T.cd[:], T.pcf[:, 2:3], A.is_equal))
+    V([("csf", 0, 3)], [("nsl", 0, 3)], v1(T.nsl[:, 0:3], T.csf[:, 0:3], -1.0, A.mult))
+    V([("pcf", 1, 2)], [("pcf", 3, 4)], v1(T.pcf[:, 3:4], T.pcf[:, 1:2], float(W), A.add))
+    for t in range(3):
+        V([("pcf", 1, 2)], [("pcf", 4 + t, 5 + t)], v1(T.pcf[:, 4 + t:5 + t], T.pcf[:, 1:2], float(t), A.is_equal))
+    for k in range(16):
+        S([full("bo")], [("sel16", 128 * k, 128 * k + 128)],
+          lambda k=k: s.activation(T.sel16[:, 128 * k + k:128 * k + 128:16], T.bo[:, 0:128:16], AF.Copy))
+    copy(col("a0u"), col(("pk", 1344)))
+
+    def more_constants():
+        V([full("bo")], [full("nb")], v1(T.nb[:], T.bo[:], -17.0, A.mult))
+        fill("rm", 0, E, 1.0)
+        V([full("rm")], [full("rm")], lambda: v.memset(T.rm[:, 0:E:16], 0.0))
+
+    def second_package():
+        V([full("pvi")], [full("pvo")], vc(T.pvo[:, 0:24:2], T.pvi[:]))
+        for c in range(12):
+            V([full("pvo"), full("pk")], [("a1f", c, c + 1)], vc(T.a1f[:, c:NL:12], T.pk[:, 0:1536].indirect(T.pvo[:, 2 * c:2 * c + 1])))
+        V([full("a1f")], [full("a1u")], vc(T.a1u[:], T.a1f[:]))
+
+    ODD, EVEN = 1, 0
+    BANK_OF = [0, 1, 0, 1, 0, 1]
+
+    def step1(tab, low, tu, tn, a0u, a0n, a1u, a1n, bias, q, t2u, filler, claims=None):
+        def lanes(x, j):
+            return col(x, CUTS[j], CUTS[j + 1])
+
+        def items(b, j):
+            return col(b, 16 * CUTS[j], 16 * CUTS[j + 1])
+
+        def xg(tr, lst, j):
+            l, o = lanes(lst, j), items("xs%d" % tr, j)
+            S([full(tab), l[1], (bias[0], bias[1], bias[1] + 1)], [o[1]],
+              lambda: s.activation(o[0], T[tab][:, 0:W].indirect(l[0]), AF.Identity, bias=T[bias[0]][:, bias[1]:bias[1] + 1]))
+
+        def compare(tr, lst, j):
+            l, x, o, n = lanes(lst, j), items("xs%d" % tr, j), items("ind", j), CUTS[j + 1] - CUTS[j]
+            V([full(tab), l[1], x[1]], [o[1]], vt(o[0], T[tab][:, 0:W].indirect(l[0]), x[0], A.is_lt if low else A.is_gt))
+            cn = "cn%d" % BANK_OF[tr * 3 + j]
+            run("p", [o[1], full("sel16")], [(cn, 0, n)],
+                *[(lambda k=k: te.matmul(T[cn][:, 0:n], T.sel16[:, 128 * k:128 * k + 128], T.ind[:, o[1][1] + k:o[1][2]:16],
+                                         k == 0, k == 15)) for k in range(16)])
+
+        def choose(tr, j):
+            n = CUTS[j + 1] - CUTS[j]
+            cn, mk = "cn%d" % BANK_OF[tr * 3 + j], "mk%d" % tr
+            src, out, lst = ("at", "tt", "t1u") if tr == 0 else ("tt", q, t2u)
+            m, u = lanes((mk, ODD, 2), j), lanes(lst, j)
+            (k, rk), (i, ri), (o, ro) = [col(b, 2 * CUTS[j], 2 * CUTS[j + 1]) for b in (mk, src, out)]
+            new = lanes((out, ODD, 2), j)
+            V([(cn, 0, n)], [m[1]], v1(m[0], T[cn][:, 0:n], 8.5, A.is_ge))
+            V([rk, ri], [ro], lambda: v.tensor_tensor_scan(o, k, i, 0.0, A.mult, A.add))
+            copy(u, new)
+            if tr == 0:
+                a, d = lanes(a1n, j), lanes((out, EVEN, 2), j)
+                V([a[1], ro], [ro], vt(d[0], a[0], new[0], A.subtract))
+
+        def rows(j):
+            if claims is not None:
+                claim_rows(claims, (q, ODD, 2), CUTS[j], CUTS[j + 1])
+
+        for j in range(3):
+            xg(0, tu, j)
+        if not low:
+            plain(6)
+            plain(7)
+        t, a = col(tn), col(a0n)
+        V([t[1]], [("at", 1, 384)], vc(T.at[:, 1:384:2], t[0]))
+        V([a[1], t[1]], [("at", 0, 383)], vt(T.at[:, 0:383:2], a[0], t[0], A.subtract))
+        filler[0]()
+        compare(0, a0u, 0)
+        filler[1]()
+        compare(0, a0u, 1)
+        choose(0, 0)
+        xg(1, "t1u", 0)
+        compare(0, a0u, 2)
+        choose(0, 1)
+        xg(1, "t1u", 1)
+        compare(1, a1u, 0)
+        choose(0, 2)
+        xg(1, "t1u", 2)
+        compare(1, a1u, 1)
+        choose(1, 0)
+        final_x(tab, low, t2u, 0)
+        rows(0)
+        compare(1, a1u, 2)
+        choose(1, 1)
+        final_x(tab, low, t2u, 1)
+        rows(1)
+        filler[2]()
+        choose(1, 2)
+        rows(2)
+        final_x(tab, low, t2u, 2)
+
+    def final_x(tab, low, t2u, j):
+        kw = {} if low else {"scale": -1.0, "bias": MAGIC + 255.0}
+        l, o = col(t2u, CUTS[j], CUTS[j + 1]), col("x2", 16 * CUTS[j], 16 * CUTS[j + 1])
+        S([full(tab), l[1]], [o[1]], lambda: s.activation(o[0], T[tab][:, 0:W].indirect(l[0]), AF.Identity, **kw))
+
+    def scan(j):
+        x, r, o = [col(b, 16 * CUTS[j], 16 * CUTS[j + 1]) for b in ("x2", "rm", "sc")]
+        V([x[1], r[1]], [o[1]], lambda: v.tensor_tensor_scan(o[0], r[0], x[0], 0.0, A.mult, A.max))
+
+    def lots_of(q):
+        S([(q, 0, 384)], [full("tf")], lambda: s.activation(T.tf[:], T[q][:, 1:384:2], AF.Identity))
+
+    def shifted(t, q):
+        S([(q, 0, 384)], [full("tc")], lambda: s.activation(T.tc[:], T[q][:, 1:384:2], AF.Identity, bias=77.0 * (t + 1)))
+
+    def weigh(wt):
+        run("p", [full("sc"), full(wt)], [("cn1", 0, NL)], lambda: te.matmul(T.cn1[:, 0:NL], T[wt][:], T.sc[:, 15:E:16], True, True))
+
+    def next_lots(q, tnu):
+        o, w, t2 = col(tnu), col("vs"), col((q, ODD, 2))
+        return [lambda: V([("cn1", 0, NL)], [full("ui")], vc(T.ui[:], T.cn1[:, 0:NL])),
+                lambda: V([full("ui")], [full("uj")], v1(T.uj[:], T.ui[:], 1023, A.bitwise_and)),
+                lambda: V([full("uj")], [w[1]], v2(w[0], T.uj[:], 2.0, 1.0, A.mult, A.add)),
+                lambda: V([w[1], t2[1]], [full("pr")], vt(T.pr[:], w[0], t2[0], A.mult)),
+                lambda: V([full("pr")], [full("ps")], v1(T.ps[:], T.pr[:], 5, A.logical_shift_right)),
+                lambda: V([full("ps"), full("tc")], [full("sm")], vt(T.sm[:], T.ps[:], T.tc[:], A.add)),
+                lambda: V([full("sm")], [full("tn")], v1(T.tn[:], T.sm[:], 4095, A.bitwise_and)),
+                lambda: V([full("tn")], [o[1]], vc(o[0], T.tn[:]))]
+
+    def bound_sums():
+        run("p", [full("mk0"), full("mk1"), full("bo"), full("nb")], [("cn1", 0, NL)],
+            lambda: te.matmul(T.cn1[:, 0:NL], T.bo[:], T.mk0[:, 1:384:2], True, False),
+            lambda: te.matmul(T.cn1[:, 0:NL], T.nb[:], T.mk1[:, 1:384:2], False, True))
+
+    def bound_sel():
+        V([("cn1", 0, NL)], [full("sel")], v1(T.sel[:], T.cn1[:, 0:NL], 0.5, A.is_ge))
+
+    def pick(first, second, out, c0):
+        f, z, o, d = col(first), col(second), col(out), col(("vs", c0))
+        return [lambda: V([f[1], z[1]], [d[1]], vt(d[0], f[0], z[0], A.subtract)),
+                lambda: V([d[1], full("sel")], [d[1]], vt(d[0], d[0], T.sel[:], A.mult)),
+                lambda: V([d[1], z[1]], [o[1]], vt(o[0], d[0], z[0], A.add))]
+
+    def claim_rows(t, t2, lo, hi):
+        x = col(t2, lo, hi)
+        run("p", [full("oneb")], [("vs", lo, hi)], lambda: te.matmul(T.vs[:, lo:hi], T.oneb[0:1, 0:128], T.oneb[0:1, 0:hi - lo], True, False))
+        run("p", [x[1], full("ts")], [("vs", lo, hi)], lambda: te.matmul(T.vs[:, lo:hi], T.ts[:, 128 * t:128 * t + 128], x[0], False, True))
+
+    def claim_list(t):
+        rm = ("rm", 0, NL)
+        return [
+            lambda: V([("vs", 0, NL), full("dm")], [full("cmk")], vt(T.cmk[:], T.vs[:, 0:NL], T.dm[:], A.mult)),
+            lambda: V([full("cmk"), rm], [full("cs1")], lambda: v.tensor_tensor_scan(T.cs1[:], T.rm[:, 0:NL], T.cmk[:], 0.0, A.mult, A.add)),
+            lambda: V([("vs", 0, NL), full("cs1")], [full("cse")], vt(T.cse[:], T.vs[:, 0:NL], T.cs1[:], A.is_equal)),
+            lambda: V([full("cse"), rm], [full("cs2")], lambda: v.tensor_tensor_scan(T.cs2[:], T.rm[:, 0:NL], T.cse[:], 0.0, A.mult, A.add)),
+            lambda: V([full("cs2")], [full("ct1")], v2(T.ct1[:], T.cs2[:, 15:NL:16], 8192.0, -8193.0, A.mult, A.add)),
+            lambda: V([full("ct1"), full("cs1")], [full("ct2")], vt(T.ct2[:], T.ct1[:], T.cs1[:, 15:NL:16], A.add))] + (
+            [lambda: V([full("ct2"), full("pcf")], [full("vl")], v1(T.vl[:], T.ct2[:], T.pcf[:, 3:4], A.min))] if t == 0 else []) + [
+            lambda: V([full("ct2"), full("pcf")], [full("of")], v1(T.of[:, 0:24:2], T.ct2[:], T.pcf[:, 3:4], A.min))]
+
+    def scatter(t):
+        w = "w%d" % t
+
+        def call(c):
+            if t == 0:
+                src, rg = col("v0", 16 * c, 16 * c + 16)
+            else:
+                src, rg = T.x2[:, 256 * c + t:256 * c + 256:16], ("x2", 256 * c, 256 * c + 256)
+            V([rg, full("of")], [(w, 0, WW)], vc(T[w][:, 0:WW].indirect(T.of[:, 2 * c:2 * c + 1]), src))
+        return [lambda c=c: call(c) for c in range(12)]
+
+    def bank(i):
+        return ["db0", "db1", "db2", "db3", "db4", "cn0", "cn1", "vs"][i]
+
+    def before(t, i, parts=(0, 1)):
+        db, lo, hi = bank(i), 512 * i, 512 * i + 512
+        k = 2 if t == 0 else 1
+        cs, (m, b) = ("cst2" if t == 0 else "cstb"), (("nid", "pl") if t == 0 else ("idm", "c"))
+        if 0 in parts:
+            run("p", [full(cs), full("oneb")], [(db, 0, 512)], lambda: te.matmul(T[db][:], T[cs][0:k, :], T.oneb[0:k, :], True, False))
+        if 1 in parts:
+            run("p", [(b, lo, hi), full(m)], [(db, 0, 512)], lambda: te.matmul(T[db][:], T[m][:], T[b][:, lo:hi], False, False))
+
+    def sums(t):
+        for i in range(8):
+            db, w = bank(i), "w%d" % t
+            run("p", [(w, 0, WW), full("qm")], [(db, 0, 512)],
+                lambda: te.matmul(T[db][:], T.qm[:], T[w][:, 512 * i:512 * i + 512], False, True))
+
+    def rise(i):
+        db, lo, hi = bank(i), 512 * i, 512 * i + 512
+        V([(db, 0, 512)], [("dd", lo, hi)], v2(T.dd[:, lo:hi], T[db][:], 0.0, MAGIC, A.max, A.add))
+
+    def plain(i):
+        lo, hi = 512 * i, 512 * i + 512
+        S([("dd", lo, hi)], [("c", lo, hi)], lambda: s.activation(T.c[:, lo:hi], T.dd[:, lo:hi], AF.Identity, bias=-MAGIC))
+
+    send_wide("pri")
+    send("cst")
+    step1("ph", True, "tu0", "lt", "a0u", ("pk", 1344), "a1u", "a1f", ("nsl", 0), "q0", "t2u0",
+          [more_constants, second_package, lambda: scan(0)])
+    stage("t2", T.t2u0, [full("t2u0")])
+    send("t2")
+    shifted(0, "q0")
+    lots_of("q0")
+    take("y", "cst", T.cso[:], [full("cso")])
+    take("y", "t2", T.o2u[:], [full("o2u")])
+    dma("y", T.yh[:, 0:NL], T.tf[:], [full("tf")], [])
+    bound_sums()
+    bound_sel()
+    weave(pick(("pk", 1344), "a1f", "b1f", 0), pick("pb0", "pnr", "par0", NL))
+    copy(col(("m4u", NL)), col("b1f"))
+    copy(col(("m4u", 2 * NL)), col("par0"))
+    copy(col("csf", 3, 8), col("cs", 3, 8))
+    scan(1)
+    V([full("bo"), ("csf", 3, 8)], [full("wth")], v1(T.wth[:], T.bo[:], T.csf[:, 4:5], A.mult))
+    scan(2)
+    weigh("wth")
+
+    def c_dm():
+        V([("pcf", 1, 2), full("cm")], [full("dm")], v1(T.dm[:], T.cm[:], T.pcf[:, 1:2], A.is_equal))
+
+    def c_eq():
+        V([("pcf", 1, 2), full("cm")], [full("eq")], v1(T.eq[:], T.cm[:, 0:128], T.pcf[:, 1:2], A.is_equal))
+
+    def c_id():
+        V([full("eq"), full("bo")], [full("idm")], vt(T.idm[:], T.eq[:], T.bo[:], A.mult))
+
+    def c_qk():
+        V([full("eq"), full("idm")], [full("qk")], vt(T.qk[:], T.eq[:], T.idm[:], A.subtract))
+
+    def c_ts(t):
+        V([full("bo"), ("pcf", 4 + t, 5 + t)], [("ts", 128 * t, 128 * t + 128)],
+          v1(T.ts[:, 128 * t:128 * t + 128], T.bo[:], T.pcf[:, 4 + t:5 + t], A.mult))
+    weave([c_eq, c_dm, c_id, lambda: c_ts(0), c_qk, lambda: fill("cstb", 0, 128, 63.0 / 128.0), lambda: fill("oneb", 0, 512, 1.0)],
+          next_lots("q0", ("m4u", 0)))
+    stage("m4", T.m4u, [full("m4u")])
+    send("m4")
+    for w in ("w1", "w2"):
+        iota(w, 0, WW, [[0, WW]], 0, 0, **small)
+    take("s", "pri", T.pl[:, 0:W], [("pl", 0, W)])
+    copy(col("cof", 0, 8), col("cso", 0, 8))
+    fill("pl", W, WW, 0.0)
+    V([full("idm"), full("cof")], [full("dg")], v2(T.dg[:], T.idm[:], T.cof[:, 3:4], -1.0 / 64.0, A.mult, A.mult))
+    run("p", [full("qk"), full("dg")], [("cn1", 0, 128)], lambda: te.matmul(T.cn1[:, 0:128], T.qk[:], T.dg[:], True, True))
+    V([full("idm")], [full("nid")], v1(T.nid[:], T.idm[:], -1.0, A.mult))
+    fill("cst2", 0, 128, 63.0 / 128.0)
+    V([], [full("cst2")], lambda: v.memset(T.cst2[0:1, :], 255.0))
+    c_ts(1)
+    c_ts(2)
+    V([full("bo"), full("cof")], [full("wto")], v1(T.wto[:], T.bo[:], T.cof[:, 4:5], A.mult))
+    V([("cn1", 0, 128)], [full("qm")], vc(T.qm[:], T.cn1[:, 0:128]))
+    for i in range(7):
+        before(0, i, (0,))
+    copy(col("o2f"), col("o2u"))
+    claim_rows(0, "o2f", 0, NL)
+    weave(claim_list(0))
+    S([("pl", 0, WW), full("vl")], [full("v0")], lambda: s.activation(T.v0[:], T.pl[:, 0:WW].indirect(T.vl[:, 0:12]), AF.Identity))
+    for i in range(8):
+        before(0, i, (1,) if i < 7 else (0, 1))
+    weave(scatter(0))
+    take("y", "m4", T.mo[:], [full("mo")])
+    sums(0)
+    for i in range(8):
+        rise(i)
+        if i < 6:
+            plain(i)
+    copy(col("mof", 0, 384), col(("mo", NL), 0, 384))
+    dma("y", T.yv[:, 0:NL], T.par0[0:128:16, :], [full("par0")], [])
+    for i in range(5):
+        before(1, i)
+    step1("dd", False, "mo", "mo", "o2u", "o2f", ("mo", NL), "mof", ("cof", 1), "q1", "t2u1", [nothing, nothing, lambda: scan(0)], 1)
+    shifted(1, "q1")
+    lots_of("q1")
+    stage("y1", T.tf, [full("tf")])
+    send("y1")
+    scan(1)
+    cl = claim_list(1)
+    weave(cl[:4])
+    scan(2)
+    weigh("wto")
+    weave(cl[4:])
+    before(1, 5)
+    weave(scatter(1), [nothing, nothing] + next_lots("q1", "tnu"))
+    before(1, 6)
+    before(1, 7)
+    sums(1)
+    for i in range(8):
+        rise(i)
+        if i < 6:
+            plain(i)
+    bound_sums()
+    bound_sel()
+    weave(pick("o2f", "mof", "b1f", 0), pick("pb1", ("mof", NL), "par12", NL))
+    copy(col("b1u"), col("b1f"))
+    take("y", "y1", T.yh[:, NL:2 * NL], [])
+    for i in range(5):
+        before(2, i)
+    step1("dd", False, "tnu", "tn", "t2u1", ("q1", ODD, 2), "b1u", "b1f", ("cof", 2), "q2", "t2u2", [nothing, nothing, nothing], 2)
+    lots_of("q2")
+    stage("y2", T.tf, [full("tf")])
+    send("y2")
+    bound_sums()
+    weave(claim_list(2))
+    before(2, 5)
+    weave(scatter(2), [nothing, bound_sel] + pick("pb2", "par12", ("par12", NL), 0))
+    before(2, 6)
+    before(2, 7)
+    stage("par", T.par12, [full("par12")], rows=True)
+    send("par")
+    sums(2)
+
+    def price(i):
+        lo, hi = 512 * i, 512 * i + 512
+        if i < 7:
+            S([("dd", lo, hi)], [("pf", lo, hi)], lambda: s.activation(T.pf[:, lo:hi], T.dd[:, lo:hi], AF.Identity, scale=-1.0, bias=MAGIC + 255.0))
+        else:
+            V([("dd", lo, hi)], [("pf", lo, hi)], v2(T.pf[:, lo:hi], T.dd[:, lo:hi], -1.0, MAGIC + 255.0, A.mult, A.add))
+
+    def ship(b):
+        p, rp = col("pf", BLOCKS[b], BLOCKS[b + 1])
+        m = "o%d" % b
+        dma("y", T["s_" + m][:], p, [rp], [full("s_" + m)])
+        dma("y", T["l_" + m][rank], T.pf[mine, BLOCKS[b]:BLOCKS[b + 1]], [rp], [full("l_" + m)])
+        send(m)
+    nxt = 0
+    for i in range(8):
+        rise(i)
+        price(i)
+        if BLOCKS[nxt + 1] <= 512 * i + 512:
+            ship(nxt)
+            nxt += 1
+    take("s", "y2", T.yh[:, 2 * NL:3 * NL], [])
+    take("s", "par", T.yv[:, NL:3 * NL], [])
+    for b in range(NB):
+        take("s", "o%d" % b, T.yp[:, BLOCKS[b]:BLOCKS[b + 1]], [])
+    for sem in sorted(total):
+        if seen.get(sem, 0) < total[sem]:
+            wait("g", sem, total[sem])

@@ -5,34 +5,60 @@ from concourse.mybir import dt, AluOpType, AxisListType, ActivationFunctionType
 A = AluOpType
 AF = ActivationFunctionType
 MAGIC = 12582912.0
+HALF = 63.0 / 128.0
 NL = 192
 E = 16 * NL
 W = 4096
 WW = W + 16
 CUTS = [0, 64, 128, 192]
-BLOCKS = [0, 1024, 2048, 3072, 3584, W]
+NC = len(CUTS) - 1
+GROUPS = [(0, 2), (2, 3)]
+HALVES = 2
+BLOCKS = [0, 1024, 2048, 3072, W]
 NB = len(BLOCKS) - 1
+FIRST = [0, 2048, W]
+RISE = ["svsvsvsv", "ssssssss", "svsvsvsv"]
+DBS = ["45670123", "45673245", "45673245"]
+APART = {}
+CYCLE, PE_CYCLE, GATHER, SCATTER, WAKE = 1.0e-3, 0.5e-3, 1.6, 3.8, 0.1
+DMA_BYTE, SEND_ISSUE, SEND_BYTE = 2.5e-6, 1.2, 0.8e-5
+START = {"run": 0.0, "dma": 2.8, "send": 3.5}
+EAGER = 10.0
+PASSES = 8
 SCRATCH = {}
+PIECE = {}
+ORDER = []
 for _d, _n, _names in (
-        ("bfloat16", W, "ph c pf"), ("bfloat16", WW, "w0 w1 w2 pl"), ("float32", W, "dd"), ("int32", 1536, "pk"),
-        ("int32", NL, "lt pnr ui uj pr ps sm tn"), ("int32", 12, "pvi"), ("uint16", 24, "pvo of"), ("uint16", 12, "vl"),
-        ("int32", 8, "cs cso pci"), ("float32", 8, "csf nsl cof pcf"), ("float32", 128, "cd"), ("float32", 384, "ts par12 at tt q0 q1 q2"),
-        ("bfloat16", 128, "bo nb eq idm nid qk dg qm wth wto cstb cst2"), ("bfloat16", 512, "oneb"), ("bfloat16", 2048, "sel16"),
-        ("bfloat16", E, "rm ind x2 sc"), ("float32", E, "xs0 xs1"), ("bfloat16", NL, "cse v0"), ("bfloat16", 384, "mk0 mk1"),
-        ("float32", NL, "cm dm pb0 pb1 pb2 a1f sel tf o2f par0 b1f tc cmk cs1 cs2"),
-        ("uint16", NL, "tu0 a0u a1u t1u t2u0 t2u1 t2u2 o2u b1u tnu"), ("float32", 12, "ct1 ct2"),
-        ("uint16", 576, "m4u mo"), ("float32", 384, "mof")):
-    for _k in _names.split():
-        SCRATCH[_k] = ("sbuf", [128, _n], _d)
+        ("bfloat16", W, "ph c1 c2 pf pl"), ("bfloat16", WW, "w0 w1 w2"), ("int32", 1536, "pk"),
+        ("int32", NL, "lt ui uj pr sm tn"), ("int32", 12, "pvi"), ("int32", 24, "mi"), ("uint16", 24, "pvo"), ("uint16", 12, "pvu"),
+        ("int32", 8, "cs cso pci"), ("float32", 8, "pcf"), ("float32", 10, "csf cof"), ("int32", 48, "si"), ("float32", 128, "cd cq cm"),
+        ("float32", 384, "tt qa qb q0 q1 q2 b0 bh b1"), ("float32", 16, "lo hi"),
+        ("bfloat16", 128, "bo nb b17 eq idm nid id64 qk dg qm qp wth wto cstb cstm cst2 cst3 zz z2"), ("bfloat16", 512, "oneb"),
+        ("bfloat16", 2048, "sel16 selw xb yb"), ("float16", 2048, "dm"), ("float16", 128, "idh"), ("float16", 12, "lh"), ("float16", NL, "a1h"),
+        ("bfloat16", E, "ind0 ind1 x2 sc"), ("bfloat16", 1536, "rm"), ("float32", E, "ys0 ys1"), ("bfloat16", NL, "vv tri in2"),
+        ("bfloat16", 384, "mk0 mk1 sp"), ("float32", 576, "ym"), ("bfloat16", 576, "im"),
+        ("float32", NL, "cm2 tf0 tf1 tf2"), ("uint16", 64, "ml0 ml1 ml2"), ("float32", 48, "mf mm"), ("float32", 24, "md pq pq2 prod"),
+        ("uint16", 40, "cl0 cl1 cl2 clo"), ("float32", 12, "pbz pb0 pb1 pb2 hh pd ps pe par0 par1 par2 pm1 pm2"),
+        ("uint16", NL, "tu0 a0u a1u t1u"), ("uint16", 512, "ma mao"), ("uint16", 256, "mb mbo")):
+    _ks = _names.split()
+    if (_d, _n) in (("bfloat16", 128), ("float32", 24), ("float32", 12)):
+        SCRATCH["side%d" % _n] = ("sbuf", [128, _n * len(_ks)], _d)
+        for _i, _k in enumerate(_ks):
+            PIECE[_k] = ("side%d" % _n, _n * _i, _n * _i + _n)
+    else:
+        for _k in _ks:
+            SCRATCH[_k] = ("sbuf", [128, _n], _d)
 MSG = []
-for _k, _n, _d in [("cst", 1, "int32"), ("pri", 512, "bfloat16"), ("t2", 24, "uint16"), ("m4", 72, "uint16"), ("y1", 24, "float32"),
-                   ("y2", 24, "float32"), ("par", 3, "float32")] + [("o%d" % _b, (BLOCKS[_b + 1] - BLOCKS[_b]) // 8, "bfloat16") for _b in range(NB)]:
+for _k, _n, _d in ([("cst", 1, "int32"), ("cl", 5, "uint16"), ("ma", 64, "uint16"), ("mb", 32, "uint16"), ("mc", 64, "uint16"), ("md", 32, "uint16")]
+                   + [(_x + "%d" % _b, (FIRST[_b + 1] - FIRST[_b]) // 8, "bfloat16") for _b in range(len(FIRST) - 1) for _x in "pk"]
+                   + [("o%d" % _b, (BLOCKS[_b + 1] - BLOCKS[_b]) // 8, "bfloat16") for _b in range(NB)]):
     MSG.append(_k)
     SCRATCH["s_" + _k] = SCRATCH["l_" + _k] = ("dram", [8, 128, _n], _d)
-BANKS = ["cn0", "cn1", "vs", "db0", "db1", "db2", "db3", "db4"]
+BANKS = ["cn0", "cn1", "m1", "m2", "db0", "db1", "db2", "db3"]
 for _k in BANKS:
     SCRATCH[_k] = ("psum", [128, 512], "float32")
-SEMAPHORES = ["vv", "ss", "pe", "gg", "lsem"] + ["d%d" % _i for _i in range(64)] + ["ar_" + _m for _m in MSG]
+SEMAPHORES = ["vv", "ss", "pe", "gg", "lsem"] + ["d%d" % _i for _i in range(100)] + ["ar_" + _m for _m in MSG]
+BYTES = {"bfloat16": 2, "float16": 2, "uint16": 2, "float32": 4, "int32": 4}
 
 
 def rank_program(g, core, T, topo):
@@ -50,6 +76,8 @@ def rank_program(g, core, T, topo):
     hist = {}
     total = {}
     seen = {}
+    calls = []
+    named = {}
 
     def wait(q, sem, val):
         if know[q].get(sem, 0) >= val:
@@ -60,16 +88,10 @@ def rank_program(g, core, T, topo):
         for k, n in snap.get((sem, val), {}).items():
             know[q][k] = max(know[q].get(k, 0), n)
 
-    def settle(q, reads, writes, is_dma):
+    def settle(q, reads, writes):
         for (b, lo, hi), wr in [(r, False) for r in reads] + [(w, True) for w in writes]:
-            bank = b in BANKS
             for e in hist.get(b, []):
-                over = e[0] < hi and lo < e[1]
-                if e[2] == q and not is_dma:
-                    need = over and (e[5] or (wr and bank))
-                else:
-                    need = bank or (over and (wr or e[5]))
-                if need:
+                if (e[0] < hi and lo < e[1] and (wr or e[5])) or (b in BANKS and e[2] != q):
                     wait(q, e[3], e[4])
 
     def record(q, sem, val, reads, writes):
@@ -79,71 +101,167 @@ def rank_program(g, core, T, topo):
             old = hist.get(b, [])
             hist[b] = [e for e in old if not (e[:3] == (lo, hi, q) and not e[5] and q != "d")] + [(lo, hi, q, sem, val, False)]
 
-    def run(q, reads, writes, *fns):
-        settle(q, reads, writes, False)
-        for f in fns[:-1]:
-            f()
-        sem = sem_of[q]
-        count[sem] += 1
-        val = total[sem] = count[sem]
-        fns[-1]().then_inc(T.sem[sem], 1)
-        snap[(sem, val)] = dict(know[q])
-        snap[(sem, val)][sem] = val
-        record(q, sem, val, reads, writes)
+    def name(q, kind, reads, writes, busy, late, issue):
+        me, after = len(calls), {}
+        for (b, lo, hi), wr in [(r, False) for r in reads] + [(w, True) for w in writes]:
+            for e in named.get(b, []):
+                if e[0] < hi and lo < e[1] and (wr or e[3]):
+                    after[e[2]] = after.get(e[2], False) or b != "order"
+        for (b, lo, hi) in writes:
+            named[b] = [e for e in named.get(b, []) if not (lo <= e[0] and e[1] <= hi)] + [(lo, hi, me, True)]
+        for (b, lo, hi) in reads:
+            named[b] = named.get(b, []) + [(lo, hi, me, False)]
+        calls.append({"q": q, "kind": kind, "busy": busy, "late": late, "after": after, "issue": issue,
+                      "banks": {x[0] for x in reads + writes if x[0] in BANKS}})
 
-    def dma(q, out, in_, reads, writes):
-        settle(q, reads, writes, True)
-        sem = "d%d" % count["d"]
-        count["d"] += 1
-        total[sem] = 16
-        eng[q].dma_start(out, in_).then_inc(T.sem[sem], 16)
-        snap[(sem, 16)] = dict(know[q])
-        record("d", sem, 16, reads, writes)
+    def run(q, reads, writes, busy, *fns):
+        def issue():
+            settle(q, reads, writes)
+            for f in fns[:-1]:
+                f()
+            sem = sem_of[q]
+            count[sem] += 1
+            val = total[sem] = count[sem]
+            fns[-1]().then_inc(T.sem[sem], 1)
+            snap[(sem, val)] = dict(know[q])
+            snap[(sem, val)][sem] = val
+            record(q, sem, val, reads, writes)
+        name(q, "run", reads, writes, busy, 0.0, issue)
 
-    def full(name):
-        return (name, 0, 1 << 20)
+    def dma(q, out, in_, reads, writes, size, first=None, keep=False):
+        def issue():
+            if first is not None:
+                first()
+            settle(q, reads, writes)
+            sem = "d%d" % count["d"]
+            count["d"] += 1
+            total[sem] = 16
+            eng[q].dma_start(out, in_).then_inc(T.sem[sem], 16)
+            snap[(sem, 16)] = dict(know[q])
+            record("d", sem, 16, reads, writes)
+        name(q, "dma", reads, writes + ([("order", "ys".index(q), "ys".index(q) + 1)] if keep else []), 0.06, size * DMA_BYTE, issue)
 
-    def col(x, lo=0, hi=NL):
-        if x in SCRATCH:
+    def place(rank_of, after, lead, forward):
+        n = len(calls)
+        follow = [[] for c in calls]
+        for i in range(n):
+            for k in after[i]:
+                follow[k].append(i)
+        left = [len(a) for a in after]
+        ready = {q: [i for i in range(n) if left[i] == 0 and calls[i]["q"] == q] for q in eng}
+        free, line, lead = {q: 0.0 for q in eng}, {"dma": 0.0, "send": 0.0}, list(lead)
+        order, done, used = [], [0.0] * n, {}
+
+        def next_of(q):
+            at = {i: max([free[q], lead[i]] + [used[b][1] + WAKE for b in calls[i]["banks"] if used.get(b, (q,))[0] != q]) for i in ready[q]}
+            i = min(at, key=lambda k: (rank_of[k] + EAGER * at[k], k))
+            return at[i], i
+        for step in range(n):
+            t, i = min(next_of(q) for q in eng if ready[q])
+            c = calls[i]
+            order.append(i)
+            free[c["q"]] = done[i] = t + c["busy"]
+            if forward and c["kind"] != "run":
+                line[c["kind"]] = max(line[c["kind"]], done[i]) + c["late"]
+                done[i] = line[c["kind"]] + START[c["kind"]]
+            for b in c["banks"]:
+                used[b] = (c["q"], done[i])
+            ready[c["q"]].remove(i)
+            for k in follow[i]:
+                if after[k][i] is not None:
+                    lead[k] = max(lead[k], done[i] + after[k][i])
+                left[k] -= 1
+                if left[k] == 0:
+                    ready[calls[k]["q"]].append(k)
+        return order, done
+
+    def find_order():
+        n = len(calls)
+        late = [c["late"] + START[c["kind"]] for c in calls]
+        ahead = [{k: WAKE if hard else None for k, hard in c["after"].items()} for c in calls]
+        back = [{} for c in calls]
+        for i in range(n):
+            for k, hard in calls[i]["after"].items():
+                back[k][i] = WAKE + late[k] if hard else None
+        rank_of, best = [0.15 * i for i in range(n)], None
+        for k in range(PASSES):
+            order, done = place(rank_of, ahead, [0.0] * n, True)
+            if best is None or max(done) < best[0]:
+                best = (max(done), order)
+            rank_of = [-t for t in place([-t for t in done], back, late, False)[1]]
+        ORDER.extend(best[1])
+
+    def full(b):
+        return PIECE.get(b, (b, 0, 1 << 20))
+
+    def col(x, lo=0, hi=NL, rows=128):
+        if isinstance(x, str):
             x = (x, 0)
-        b, st = x[0], x[2] if len(x) > 2 else 1
-        i, j = x[1] + lo * st, x[1] + (hi - 1) * st + 1
-        return (T[b][:, i:j] if st == 1 else T[b][:, i:j:st]), (b, i, j)
+        (b, first), st = PIECE.get(x[0], (x[0], 0))[:2], x[2] if len(x) > 2 else 1
+        i, j = first + x[1] + lo * st, first + x[1] + (hi - 1) * st + 1
+        return (T[b][0:rows, i:j] if st == 1 else T[b][0:rows, i:j:st]), (b, i, j), hi - lo
 
-    def V(reads, writes, f):
-        run("v", reads, writes, f)
-
-    def S(reads, writes, f):
-        run("s", reads, writes, f)
+    def pick(tab, lst, n=W):
+        return (T[tab][:, 0:n].indirect(lst[0]), (tab, 0, n), 16 * lst[2], lst[1])
 
     v, s, te = g.vector, g.scalar, g.tensor
 
-    def vt(out, in0, in1, op):
-        return lambda: v.tensor_tensor(out, in0, in1, op)
+    def val(x):
+        return x[0] if isinstance(x, tuple) else x
 
-    def vc(out, in_):
-        return lambda: v.tensor_copy(out, in_)
+    def rd(o, *xs):
+        return [x[1] for x in xs if isinstance(x, tuple)] + [x[3] for x in (o,) + xs if isinstance(x, tuple) and len(x) > 3]
 
-    def v1(out, in0, s1, op):
-        return lambda: v.tensor_scalar(out, in0, s1, None, op)
+    def width(x):
+        return BYTES[SCRATCH[x[1][0]][2]]
 
-    def v2(out, in0, s1, s2, op0, op1):
-        return lambda: v.tensor_scalar(out, in0, s1, s2, op0, op1)
+    def lasts(o, a, *more, per=None):
+        if len(o) > 3 or len(a) > 3:
+            return 0.06 + o[2] * CYCLE * (SCATTER if len(o) > 3 else GATHER)
+        return max(64, o[2] * (per or (0.5 if max(width(x) for x in (o, a) + more) == 2 else 1))) * CYCLE
 
-    def copy(out, in_):
-        V([in_[1]], [out[1]], vc(out[0], in_[0]))
+    def tt(o, a, b, op):
+        run("v", rd(o, a, b), [o[1]], lasts(o, a, per=1 if a[1][0] in BANKS or b[1][0] in BANKS else 2), lambda: v.tensor_tensor(o[0], a[0], b[0], op))
 
-    def fill(b, lo, hi, x):
-        V([], [(b, lo, hi)], lambda: v.memset(T[b][:, lo:hi], x))
+    def cp(o, a):
+        run("v", rd(o, a), [o[1]], lasts(o, a), lambda: v.tensor_copy(o[0], a[0]))
 
-    def weave(*chains):
-        for i in range(max(len(c) for c in chains)):
-            for c in chains:
-                if i < len(c):
-                    c[i]()
+    def ts(o, a, s1, op0, s2=None, op1=None):
+        if op1 is None:
+            run("v", rd(o, a, s1), [o[1]], lasts(o, a), lambda: v.tensor_scalar(o[0], a[0], val(s1), None, op0))
+        else:
+            run("v", rd(o, a, s1, s2), [o[1]], lasts(o, a), lambda: v.tensor_scalar(o[0], a[0], val(s1), val(s2), op0, op1))
 
-    def nothing():
-        pass
+    def scan2(o, d0, d1, op1):
+        run("v", rd(o, d0, d1), [o[1]], lasts(o, d0, d1), lambda: v.tensor_tensor_scan(o[0], d0[0], d1[0], 0.0, A.mult, op1))
+
+    def act(o, a, f=AF.Identity, **kw):
+        run("s", rd(o, a, *kw.values()), [o[1]], 0.06 + lasts(o, a, per=1), lambda: s.activation(o[0], a[0], f, **{k: val(x) for k, x in kw.items()}))
+
+    def fill(b, lo, hi, x, rows=128):
+        o = col(b, lo, hi, rows)
+        run("v", [], [o[1]], lasts(o, o), lambda: v.memset(o[0], x))
+
+    def mm(out, terms, start=True, stop=True):
+        outs = out if isinstance(out, list) else [out] * len(terms)
+        last = len(terms) - 1
+        run("p", [x[1] for t in terms for x in t], [o[1] for o in outs], sum(max(64, o[2]) for o in outs) * PE_CYCLE,
+            *[(lambda k=k: te.matmul(outs[k][0], terms[k][0][0], terms[k][1][0], start and k == 0, stop and k == last)) for k in range(last + 1)])
+
+    def c128(b, k=0):
+        return col(b, 128 * k, 128 * k + 128)
+
+    def c12(b, k=0):
+        return col(b, 12 * k, 12 * k + 12)
+
+    def cols(b, i):
+        return col(b, 512 * i, 512 * i + 512)
+
+    def odd(b):
+        return (b, 1, 2)
+
+    def even(b):
+        return (b, 0, 2)
 
     others = [(rank + j) % N for j in range(1, N)]
     away = [d for d in others if topo.chip(cores[d]) != topo.chip(core)]
@@ -153,26 +271,32 @@ def rank_program(g, core, T, topo):
     turn = [0]
     arrive = {m: 0 for m in MSG}
 
-    def fused(m, plan):
-        settle("g", [full("s_" + m)], [], True)
-        tr = []
-        for d, es in plan:
-            rid, pid, _e = topo.addr(cores[d])
-            tr.append(RemoteDMATransfer(dst_ids=[DstId(rid=rid, pnc=pid)], dma_engine_mask=sum(1 << e for e in es),
-                                        remote_sem=T.sem["ar_" + m], src=T["s_" + m][d], dst=T["l_" + m][rank]))
-        g.remote_dma_fused(tr, local_sem=T.sem.lsem)
-        n = sum(len(es) for d, es in plan)
-        total["lsem"] = total.get("lsem", 0) + n
-        arrive[m] += n
+    def size_of(m):
+        return 8 * 128 * SCRATCH["s_" + m][1][2] * BYTES[SCRATCH["s_" + m][2]]
+
+    def fused(m, plan, part):
+        def issue():
+            settle("g", [full("s_" + m)], [])
+            tr, n = [], 0
+            for d, es in plan():
+                rid, pid, _e = topo.addr(cores[d])
+                tr.append(RemoteDMATransfer(dst_ids=[DstId(rid=rid, pnc=pid)], dma_engine_mask=sum(1 << e for e in es),
+                                            remote_sem=T.sem["ar_" + m], src=T["s_" + m][d], dst=T["l_" + m][rank]))
+                n += len(es)
+            g.remote_dma_fused(tr, local_sem=T.sem.lsem)
+            total["lsem"] = total.get("lsem", 0) + n
+            arrive[m] += n
+        name("g", "send", [full("s_" + m)], [("ar_" + m, part[0], part[0] + 1), ("order", 2, 3)], SEND_ISSUE, size_of(m) * SEND_BYTE / part[1], issue)
 
     def send(m):
-        plan = [(d, [offe[(turn[0] + j) % len(offe)]]) for j, d in enumerate(away)]
-        turn[0] += len(away)
-        fused(m, plan + [(d, one[0:3:2]) for d in near])
+        def plan():
+            turn[0] += len(away)
+            return [(d, [offe[(turn[0] + j) % len(offe)]]) for j, d in enumerate(away)] + [(d, one[0:3:2]) for d in near]
+        fused(m, plan, (0, 1))
 
     def send_wide(m):
-        fused(m, [(d, offe[2 * j:2 * j + 2]) for j, d in enumerate(away[:4])] + [(d, one[0:3:2]) for d in near])
-        fused(m, [(d, offe[4 * j:4 * j + 4]) for j, d in enumerate(away[4:])])
+        fused(m, lambda: [(d, offe[2 * j:2 * j + 2]) for j, d in enumerate(away[:4])] + [(d, one[0:3:2]) for d in near], (0, 2))
+        fused(m, lambda: [(d, offe[4 * j:4 * j + 4]) for j, d in enumerate(away[4:])], (1, 2))
 
     def landed(q, m):
         total["ar_" + m] = arrive[m]
@@ -180,376 +304,359 @@ def rank_program(g, core, T, topo):
 
     mine = slice(16 * rank, 16 * rank + 16)
 
-    def stage(m, in_, reads, rows=None):
-        dma("y", T["s_" + m][:], in_[:] if rows is None else in_[0:128:16, :], reads, [full("s_" + m)])
-        dma("y", T["l_" + m][rank], in_[mine, :] if rows is None else in_[16 * rank:16 * rank + 1, :], reads, [full("l_" + m)])
+    def stage(m, src, lo, hi, reads, keep=False):
+        dma("y", T["s_" + m][:], src[:, lo:hi], reads, [full("s_" + m)], size_of(m), keep=keep)
+        dma("y", T["l_" + m][rank], src[mine, lo:hi], reads, [full("l_" + m)], size_of(m) // 8, keep=keep)
 
-    def take(q, m, out, writes):
-        landed(q, m)
-        dma(q, out, T["l_" + m][:], [full("l_" + m)], writes)
+    def take(m, out, writes, rows=slice(0, 128)):
+        dma("y", out, T["l_" + m][:, rows, :], [full("l_" + m), full("ar_" + m)], writes, size_of(m) * (rows.stop - rows.start) // 128,
+            lambda: landed("y", m))
 
-    fill("cs", 0, 8, 0)
-    fill("pnr", 0, NL, 0)
-    fill("mk0", 0, 384, 0.0)
-    fill("mk1", 0, 384, 0.0)
-    dma("s", T.lt[:], T.lots[:], [], [full("lt")])
-    dma("y", T.cs[:, 0:3], T.slack[:], [], [("cs", 0, 3)])
-    dma("y", T.ph[:], T.price[:], [], [full("ph")])
-    dma("s", T.pk[:, 1344:1536], T.packs[:, 1344:1536], [], [("pk", 1344, 1536)])
-    dma("s", T.pvi[:], T.prev[:, 1344:1536], [], [full("pvi")])
-    dma("y", T.pk[:, 0:1344], T.packs[:, 0:1344], [], [("pk", 0, 1344)])
-    dma("s", T.cs[:, 3:4], T.inc[:], [], [("cs", 3, 4)])
-    dma("s", T.cs[:, 4:5], T.wt[:], [], [("cs", 4, 5)])
-    dma("s", T.pnr[0:128:16, :], T.prev[:, 1344:1536], [], [full("pnr")])
-    stage("pri", T.price, [])
-    stage("cst", T.cs, [full("cs")])
+    def load(q, o, src, size=1e5):
+        dma(q, o[0], src, [], [o[1]], size, keep=True)
+    load("y", col("lt"), T.lots[:])
+    load("s", col("pk", 1344, 1536), T.packs[:, 1344:1536])
+    load("y", col("cs", 0, 3), T.slack[:])
+    load("s", c12("pvi"), T.prev[:, 1344:1536])
+    load("y", col("ph", 0, W), T.price[:], 1e6)
+    fill("cs", 4, 8, 0)
+    load("s", c12("mi"), T.packs[0:128:16, 1344:1536])
+    load("s", c12("mi", 1), T.lots[0:128:16, :])
+    load("s", col("cs", 3, 4), T.inc[:])
+    dma("s", T.cs[:, 4:5], T.wt[:], [], [("cs", 4, 8)], 1e5, keep=True)
+    stage("p0", T.price, FIRST[0], FIRST[1], [], keep=True)
+    load("y", col("pk", 0, 1344), T.packs[:, 0:1344], 7e5)
+    for b in range(1, len(FIRST) - 1):
+        stage("p%d" % b, T.price, FIRST[b], FIRST[b + 1], [], keep=True)
+    stage("cst", T.cs, 0, 8, [full("cs")])
 
-    def iota(b, lo, hi, pat, base, cm, **kw):
-        run("g", [], [(b, lo, hi)], lambda: g.iota(T[b][:, lo:hi], pat, base, cm, **kw))
-    small = {"allow_small_or_imprecise_dtypes": True}
-    iota("pci", 0, 1, [[0, 1]], 0, 1)
-    iota("cd", 0, 128, [[1, 8], [0, 16]], 0, 0, **small)
-    iota("cm", 0, NL, [[0, 12], [1, 16]], 0, 0, **small)
-    for t in range(3):
-        iota("pb%d" % t, 0, NL, [[1, NL]], 1344 + NL * t, 0, **small)
-    iota("w0", 0, WW, [[0, WW]], 0, 0, **small)
-    V([("pci", 0, 1)], [("pci", 1, 2)], v1(T.pci[:, 1:2], T.pci[:, 0:1], 15, A.bitwise_and))
-    V([("pci", 0, 1)], [("pci", 2, 3)], v1(T.pci[:, 2:3], T.pci[:, 0:1], 4, A.logical_shift_right))
+    def iota(b, lo, hi, pat, more=()):
+        o = col(b, lo, hi)
+        run("g", list(more), [o[1]], 0.13 + 2 * o[2] * CYCLE, lambda: g.iota(o[0], pat, 0, 0, allow_small_or_imprecise_dtypes=True))
+
+    def zeros(w, more=()):
+        for k in range(8):
+            iota(w, WW * k // 8, WW * (k + 1) // 8, [[0, WW // 8]], more)
+    run("g", [], [("pci", 0, 1)], 0.13, lambda: g.iota(T.pci[:, 0:1], [[0, 1]], 0, 1))
+    iota("cd", 0, 128, [[1, 8], [0, 16]])
+    iota("cq", 0, 128, [[1, 128]])
+    iota("cm2", 0, NL, [[1, 16], [0, 12]])
+    iota("pbz", 0, 12, [[1, 12]])
+    iota("cm", 0, 128, [[0, 8], [1, 16]])
+    for k in ("mk0", "mk1", "sp"):
+        iota(k, 0, 384, [[0, 384]])
+    zeros("w0")
+    p0, p1, p2, p3 = [col("pcf", k, k + 1) for k in range(4)]
     fill("sel16", 0, 2048, 0.0)
-    V([("pci", 1, 3)], [("pcf", 1, 3)], vc(T.pcf[:, 1:3], T.pci[:, 1:3]))
-    copy(col("tu0"), col("lt"))
-    copy(col("csf", 0, 3), col("cs", 0, 3))
-    V([full("cd"), ("pcf", 2, 3)], [full("bo")], v1(T.bo[:], T.cd[:], T.pcf[:, 2:3], A.is_equal))
-    V([("csf", 0, 3)], [("nsl", 0, 3)], v1(T.nsl[:, 0:3], T.csf[:, 0:3], -1.0, A.mult))
-    V([("pcf", 1, 2)], [("pcf", 3, 4)], v1(T.pcf[:, 3:4], T.pcf[:, 1:2], float(W), A.add))
-    for t in range(3):
-        V([("pcf", 1, 2)], [("pcf", 4 + t, 5 + t)], v1(T.pcf[:, 4 + t:5 + t], T.pcf[:, 1:2], float(t), A.is_equal))
+    ts(col("pci", 1, 2), col("pci", 0, 1), 15, A.bitwise_and)
+    ts(col("pci", 2, 3), col("pci", 0, 1), 4, A.logical_shift_right)
+    widest = max(CUTS[j + 1] - CUTS[j] for j in range(NC))
+    fill("rm", 0, 16 * widest, 1.0)
+    fill(("rm", 0, 16), 0, widest, 0.0)
+    cp(col("pcf", 0, 3), col("pci", 0, 3))
+    ts(c128("bo"), c128("cd"), p2, A.is_equal)
+    ts(c128("z2"), c128("cq"), p0, A.is_equal, 2.0, A.mult)
+    ts(col("lo", 0, 16), col("cq", 0, 16), p1, A.is_equal, -1.0, A.mult)
+    ts(col("hi", 0, 16), col("cq", 0, 16), p1, A.not_equal)
     for k in range(16):
-        S([full("bo")], [("sel16", 128 * k, 128 * k + 128)],
-          lambda k=k: s.activation(T.sel16[:, 128 * k + k:128 * k + 128:16], T.bo[:, 0:128:16], AF.Copy))
-    copy(col("a0u"), col(("pk", 1344)))
+        act(col(("sel16", 129 * k, 16), 0, 8), col(("bo", 0, 16), 0, 8), AF.Copy)
+    tt(c128("zz"), c128("z2"), c128("bo"), A.subtract)
+    ts(c128("idm"), c128("cq"), p0, A.is_equal)
+    ts(c128("idh"), c128("cq"), p0, A.is_equal)
+    for r in range(16):
+        ts(c128("dm", r), c128("zz"), col("lo", r, r + 1), A.max, col("hi", r, r + 1), A.min)
+    ts(col("tri"), col("cm2"), p1, A.is_le, 8192.0, A.mult)
+    ts(p3, p1, float(W), A.add)
+    ts(col("pcf", 4, 5), p1, 12.0, A.mult, 1344.0, A.add)
+    ts(col("pcf", 5, 6), p1, 0.0, A.is_equal)
+    ts(c128("nb"), c128("bo"), -1.0, A.mult)
+    ts(c128("b17"), c128("bo"), 17.0, A.mult)
+    ts(c128("eq"), c128("cm"), p1, A.is_equal)
+    for t in range(3):
+        ts(c12("pb%d" % t), c12("pbz"), col("pcf", 4, 5), A.add, float(NL * t), A.add)
+        fill("cl%d" % t, 0, 40, 0)
+    fill("ma", 384, 512, 0)
+    fill("mb", NL, 256, 0)
+    tt(c128("qk"), c128("eq"), c128("idm"), A.subtract)
+    ts(c128("nid"), c128("idm"), -1.0, A.mult)
+    ts(c128("id64"), c128("idm"), -1.0 / 64.0, A.mult)
+    fill("cstb", 0, 128, HALF)
+    fill("cstm", 0, 128, MAGIC)
+    fill("cst2", 0, 128, HALF)
+    fill("cst3", 0, 128, -HALF)
+    fill("oneb", 0, 512, 1.0)
+    for k in ("cst2", "cst3"):
+        fill(k, 0, 128, 255.0, 1)
 
-    def more_constants():
-        V([full("bo")], [full("nb")], v1(T.nb[:], T.bo[:], -17.0, A.mult))
-        fill("rm", 0, E, 1.0)
-        V([full("rm")], [full("rm")], lambda: v.memset(T.rm[:, 0:E:16], 0.0))
+    def lanes(x, j):
+        j, k = j if isinstance(j, tuple) else (j, j + 1)
+        if isinstance(x, list):
+            x = (x[0], CUTS[-2] * x[2]) if j < NC - 1 else (x[1], (NL - CUTS[-2]) * x[2] - CUTS[-2])
+        return col(x, CUTS[j], CUTS[k])
 
-    def second_package():
-        V([full("pvi")], [full("pvo")], vc(T.pvo[:, 0:24:2], T.pvi[:]))
-        for c in range(12):
-            V([full("pvo"), full("pk")], [("a1f", c, c + 1)], vc(T.a1f[:, c:NL:12], T.pk[:, 0:1536].indirect(T.pvo[:, 2 * c:2 * c + 1])))
-        V([full("a1f")], [full("a1u")], vc(T.a1u[:], T.a1f[:]))
+    def items(b, j):
+        return col(b, 16 * CUTS[j], 16 * CUTS[j + 1])
 
-    ODD, EVEN = 1, 0
-    BANK_OF = [0, 1, 0, 1, 0, 1]
+    def pairs(b, j):
+        j, k = j if isinstance(j, tuple) else (j, j + 1)
+        return col(b, 2 * CUTS[j], 2 * CUTS[k])
 
-    def step1(tab, low, tu, tn, a0u, a0n, a1u, a1n, bias, q, t2u, filler, claims=None):
-        def lanes(x, j):
-            return col(x, CUTS[j], CUTS[j + 1])
+    came = dict(a0u=["mao", "mbo", 0], a1u=["mao", "mbo", 1], tu=["mao", "mbo", 2], tn=["mao", "mbo", 2], a0="qb", a1="b1")
+    goes = dict(t2u=["ma", "mb", 0], bu=["ma", "mb", 1], nu=["ma", "mb", 2])
+    R = [dict(tab="ph", tu="tu0", tn="lt", a0u="a0u", a0="qa", a1u="a1u", a1="b0", sl=("csf", 0), sg=("csf", 5), q="q0", wt="wth",
+              par=("pb0", "pvi", "par0"), **goes),
+         dict(tab="c1", sl=("cof", 5), sg=("cof", 8), q="q1", wt="wto", par=("pb1", "pm1", "par1"), **came, **goes),
+         dict(tab="ph", sl=("csf", 6), sg=("csf", 7), q="q2", par=("pb2", "pm2", "par2"), **came)]
+    counted, apart = [0], []
 
-        def items(b, j):
-            return col(b, 16 * CUTS[j], 16 * CUTS[j + 1])
+    def part(x, h):
+        b, lo, hi = x[-1] if len(x) > 3 else x[1]
+        n = (hi - lo) // HALVES
+        y = col(b, lo + n * h, lo + n * h + n)
+        return pick(x[1][0], y) if len(x) > 3 else y
 
-        def xg(tr, lst, j):
-            l, o = lanes(lst, j), items("xs%d" % tr, j)
-            S([full(tab), l[1], (bias[0], bias[1], bias[1] + 1)], [o[1]],
-              lambda: s.activation(o[0], T[tab][:, 0:W].indirect(l[0]), AF.Identity, bias=T[bias[0]][:, bias[1]:bias[1] + 1]))
-
-        def compare(tr, lst, j):
-            l, x, o, n = lanes(lst, j), items("xs%d" % tr, j), items("ind", j), CUTS[j + 1] - CUTS[j]
-            V([full(tab), l[1], x[1]], [o[1]], vt(o[0], T[tab][:, 0:W].indirect(l[0]), x[0], A.is_lt if low else A.is_gt))
-            cn = "cn%d" % BANK_OF[tr * 3 + j]
-            run("p", [o[1], full("sel16")], [(cn, 0, n)],
-                *[(lambda k=k: te.matmul(T[cn][:, 0:n], T.sel16[:, 128 * k:128 * k + 128], T.ind[:, o[1][1] + k:o[1][2]:16],
-                                         k == 0, k == 15)) for k in range(16)])
-
-        def choose(tr, j):
-            n = CUTS[j + 1] - CUTS[j]
-            cn, mk = "cn%d" % BANK_OF[tr * 3 + j], "mk%d" % tr
-            src, out, lst = ("at", "tt", "t1u") if tr == 0 else ("tt", q, t2u)
-            m, u = lanes((mk, ODD, 2), j), lanes(lst, j)
-            (k, rk), (i, ri), (o, ro) = [col(b, 2 * CUTS[j], 2 * CUTS[j + 1]) for b in (mk, src, out)]
-            new = lanes((out, ODD, 2), j)
-            V([(cn, 0, n)], [m[1]], v1(m[0], T[cn][:, 0:n], 8.5, A.is_ge))
-            V([rk, ri], [ro], lambda: v.tensor_tensor_scan(o, k, i, 0.0, A.mult, A.add))
-            copy(u, new)
-            if tr == 0:
-                a, d = lanes(a1n, j), lanes((out, EVEN, 2), j)
-                V([a[1], ro], [ro], vt(d[0], a[0], new[0], A.subtract))
-
-        def rows(j):
-            if claims is not None:
-                claim_rows(claims, (q, ODD, 2), CUTS[j], CUTS[j + 1])
-
-        for j in range(3):
-            xg(0, tu, j)
-        if not low:
-            plain(6)
-            plain(7)
-        t, a = col(tn), col(a0n)
-        V([t[1]], [("at", 1, 384)], vc(T.at[:, 1:384:2], t[0]))
-        V([a[1], t[1]], [("at", 0, 383)], vt(T.at[:, 0:383:2], a[0], t[0], A.subtract))
-        filler[0]()
-        compare(0, a0u, 0)
-        filler[1]()
-        compare(0, a0u, 1)
-        choose(0, 0)
-        xg(1, "t1u", 0)
-        compare(0, a0u, 2)
-        choose(0, 1)
-        xg(1, "t1u", 1)
-        compare(1, a1u, 0)
-        choose(0, 2)
-        xg(1, "t1u", 2)
-        compare(1, a1u, 1)
-        choose(1, 0)
-        final_x(tab, low, t2u, 0)
-        rows(0)
-        compare(1, a1u, 2)
-        choose(1, 1)
-        final_x(tab, low, t2u, 1)
-        rows(1)
-        filler[2]()
-        choose(1, 2)
-        rows(2)
-        final_x(tab, low, t2u, 2)
-
-    def final_x(tab, low, t2u, j):
-        kw = {} if low else {"scale": -1.0, "bias": MAGIC + 255.0}
-        l, o = col(t2u, CUTS[j], CUTS[j + 1]), col("x2", 16 * CUTS[j], 16 * CUTS[j + 1])
-        S([full(tab), l[1]], [o[1]], lambda: s.activation(o[0], T[tab][:, 0:W].indirect(l[0]), AF.Identity, **kw))
-
-    def scan(j):
-        x, r, o = [col(b, 16 * CUTS[j], 16 * CUTS[j + 1]) for b in ("x2", "rm", "sc")]
-        V([x[1], r[1]], [o[1]], lambda: v.tensor_tensor_scan(o[0], r[0], x[0], 0.0, A.mult, A.max))
-
-    def lots_of(q):
-        S([(q, 0, 384)], [full("tf")], lambda: s.activation(T.tf[:], T[q][:, 1:384:2], AF.Identity))
-
-    def shifted(t, q):
-        S([(q, 0, 384)], [full("tc")], lambda: s.activation(T.tc[:], T[q][:, 1:384:2], AF.Identity, bias=77.0 * (t + 1)))
-
-    def weigh(wt):
-        run("p", [full("sc"), full(wt)], [("cn1", 0, NL)], lambda: te.matmul(T.cn1[:, 0:NL], T[wt][:], T.sc[:, 15:E:16], True, True))
-
-    def next_lots(q, tnu):
-        o, w, t2 = col(tnu), col("vs"), col((q, ODD, 2))
-        return [lambda: V([("cn1", 0, NL)], [full("ui")], vc(T.ui[:], T.cn1[:, 0:NL])),
-                lambda: V([full("ui")], [full("uj")], v1(T.uj[:], T.ui[:], 1023, A.bitwise_and)),
-                lambda: V([full("uj")], [w[1]], v2(w[0], T.uj[:], 2.0, 1.0, A.mult, A.add)),
-                lambda: V([w[1], t2[1]], [full("pr")], vt(T.pr[:], w[0], t2[0], A.mult)),
-                lambda: V([full("pr")], [full("ps")], v1(T.ps[:], T.pr[:], 5, A.logical_shift_right)),
-                lambda: V([full("ps"), full("tc")], [full("sm")], vt(T.sm[:], T.ps[:], T.tc[:], A.add)),
-                lambda: V([full("sm")], [full("tn")], v1(T.tn[:], T.sm[:], 4095, A.bitwise_and)),
-                lambda: V([full("tn")], [o[1]], vc(o[0], T.tn[:]))]
-
-    def bound_sums():
-        run("p", [full("mk0"), full("mk1"), full("bo"), full("nb")], [("cn1", 0, NL)],
-            lambda: te.matmul(T.cn1[:, 0:NL], T.bo[:], T.mk0[:, 1:384:2], True, False),
-            lambda: te.matmul(T.cn1[:, 0:NL], T.nb[:], T.mk1[:, 1:384:2], False, True))
-
-    def bound_sel():
-        V([("cn1", 0, NL)], [full("sel")], v1(T.sel[:], T.cn1[:, 0:NL], 0.5, A.is_ge))
-
-    def pick(first, second, out, c0):
-        f, z, o, d = col(first), col(second), col(out), col(("vs", c0))
-        return [lambda: V([f[1], z[1]], [d[1]], vt(d[0], f[0], z[0], A.subtract)),
-                lambda: V([d[1], full("sel")], [d[1]], vt(d[0], d[0], T.sel[:], A.mult)),
-                lambda: V([d[1], z[1]], [o[1]], vt(o[0], d[0], z[0], A.add))]
-
-    def claim_rows(t, t2, lo, hi):
-        x = col(t2, lo, hi)
-        run("p", [full("oneb")], [("vs", lo, hi)], lambda: te.matmul(T.vs[:, lo:hi], T.oneb[0:1, 0:128], T.oneb[0:1, 0:hi - lo], True, False))
-        run("p", [x[1], full("ts")], [("vs", lo, hi)], lambda: te.matmul(T.vs[:, lo:hi], T.ts[:, 128 * t:128 * t + 128], x[0], False, True))
-
-    def claim_list(t):
-        rm = ("rm", 0, NL)
-        return [
-            lambda: V([("vs", 0, NL), full("dm")], [full("cmk")], vt(T.cmk[:], T.vs[:, 0:NL], T.dm[:], A.mult)),
-            lambda: V([full("cmk"), rm], [full("cs1")], lambda: v.tensor_tensor_scan(T.cs1[:], T.rm[:, 0:NL], T.cmk[:], 0.0, A.mult, A.add)),
-            lambda: V([("vs", 0, NL), full("cs1")], [full("cse")], vt(T.cse[:], T.vs[:, 0:NL], T.cs1[:], A.is_equal)),
-            lambda: V([full("cse"), rm], [full("cs2")], lambda: v.tensor_tensor_scan(T.cs2[:], T.rm[:, 0:NL], T.cse[:], 0.0, A.mult, A.add)),
-            lambda: V([full("cs2")], [full("ct1")], v2(T.ct1[:], T.cs2[:, 15:NL:16], 8192.0, -8193.0, A.mult, A.add)),
-            lambda: V([full("ct1"), full("cs1")], [full("ct2")], vt(T.ct2[:], T.ct1[:], T.cs1[:, 15:NL:16], A.add))] + (
-            [lambda: V([full("ct2"), full("pcf")], [full("vl")], v1(T.vl[:], T.ct2[:], T.pcf[:, 3:4], A.min))] if t == 0 else []) + [
-            lambda: V([full("ct2"), full("pcf")], [full("of")], v1(T.of[:, 0:24:2], T.ct2[:], T.pcf[:, 3:4], A.min))]
-
-    def scatter(t):
-        w = "w%d" % t
-
-        def call(c):
-            if t == 0:
-                src, rg = col("v0", 16 * c, 16 * c + 16)
-            else:
-                src, rg = T.x2[:, 256 * c + t:256 * c + 256:16], ("x2", 256 * c, 256 * c + 256)
-            V([rg, full("of")], [(w, 0, WW)], vc(T[w][:, 0:WW].indirect(T.of[:, 2 * c:2 * c + 1]), src))
-        return [lambda c=c: call(c) for c in range(12)]
-
-    def bank(i):
-        return ["db0", "db1", "db2", "db3", "db4", "cn0", "cn1", "vs"][i]
-
-    def before(t, i, parts=(0, 1)):
-        db, lo, hi = bank(i), 512 * i, 512 * i + 512
-        k = 2 if t == 0 else 1
-        cs, (m, b) = ("cst2" if t == 0 else "cstb"), (("nid", "pl") if t == 0 else ("idm", "c"))
-        if 0 in parts:
-            run("p", [full(cs), full("oneb")], [(db, 0, 512)], lambda: te.matmul(T[db][:], T[cs][0:k, :], T.oneb[0:k, :], True, False))
-        if 1 in parts:
-            run("p", [(b, lo, hi), full(m)], [(db, 0, 512)], lambda: te.matmul(T[db][:], T[m][:], T[b][:, lo:hi], False, False))
-
-    def sums(t):
-        for i in range(8):
-            db, w = bank(i), "w%d" % t
-            run("p", [(w, 0, WW), full("qm")], [(db, 0, 512)],
-                lambda: te.matmul(T[db][:], T.qm[:], T[w][:, 512 * i:512 * i + 512], False, True))
-
-    def rise(i):
-        db, lo, hi = bank(i), 512 * i, 512 * i + 512
-        V([(db, 0, 512)], [("dd", lo, hi)], v2(T.dd[:, lo:hi], T[db][:], 0.0, MAGIC, A.max, A.add))
-
-    def plain(i):
-        lo, hi = 512 * i, 512 * i + 512
-        S([("dd", lo, hi)], [("c", lo, hi)], lambda: s.activation(T.c[:, lo:hi], T.dd[:, lo:hi], AF.Identity, bias=-MAGIC))
-
-    send_wide("pri")
-    send("cst")
-    step1("ph", True, "tu0", "lt", "a0u", ("pk", 1344), "a1u", "a1f", ("nsl", 0), "q0", "t2u0",
-          [more_constants, second_package, lambda: scan(0)])
-    stage("t2", T.t2u0, [full("t2u0")])
-    send("t2")
-    shifted(0, "q0")
-    lots_of("q0")
-    take("y", "cst", T.cso[:], [full("cso")])
-    take("y", "t2", T.o2u[:], [full("o2u")])
-    dma("y", T.yh[:, 0:NL], T.tf[:], [full("tf")], [])
-    bound_sums()
-    bound_sel()
-    weave(pick(("pk", 1344), "a1f", "b1f", 0), pick("pb0", "pnr", "par0", NL))
-    copy(col(("m4u", NL)), col("b1f"))
-    copy(col(("m4u", 2 * NL)), col("par0"))
-    copy(col("csf", 3, 8), col("cs", 3, 8))
-    scan(1)
-    V([full("bo"), ("csf", 3, 8)], [full("wth")], v1(T.wth[:], T.bo[:], T.csf[:, 4:5], A.mult))
-    scan(2)
-    weigh("wth")
-
-    def c_dm():
-        V([("pcf", 1, 2), full("cm")], [full("dm")], v1(T.dm[:], T.cm[:], T.pcf[:, 1:2], A.is_equal))
-
-    def c_eq():
-        V([("pcf", 1, 2), full("cm")], [full("eq")], v1(T.eq[:], T.cm[:, 0:128], T.pcf[:, 1:2], A.is_equal))
-
-    def c_id():
-        V([full("eq"), full("bo")], [full("idm")], vt(T.idm[:], T.eq[:], T.bo[:], A.mult))
-
-    def c_qk():
-        V([full("eq"), full("idm")], [full("qk")], vt(T.qk[:], T.eq[:], T.idm[:], A.subtract))
-
-    def c_ts(t):
-        V([full("bo"), ("pcf", 4 + t, 5 + t)], [("ts", 128 * t, 128 * t + 128)],
-          v1(T.ts[:, 128 * t:128 * t + 128], T.bo[:], T.pcf[:, 4 + t:5 + t], A.mult))
-    weave([c_eq, c_dm, c_id, lambda: c_ts(0), c_qk, lambda: fill("cstb", 0, 128, 63.0 / 128.0), lambda: fill("oneb", 0, 512, 1.0)],
-          next_lots("q0", ("m4u", 0)))
-    stage("m4", T.m4u, [full("m4u")])
-    send("m4")
-    for w in ("w1", "w2"):
-        iota(w, 0, WW, [[0, WW]], 0, 0, **small)
-    take("s", "pri", T.pl[:, 0:W], [("pl", 0, W)])
-    copy(col("cof", 0, 8), col("cso", 0, 8))
-    fill("pl", W, WW, 0.0)
-    V([full("idm"), full("cof")], [full("dg")], v2(T.dg[:], T.idm[:], T.cof[:, 3:4], -1.0 / 64.0, A.mult, A.mult))
-    run("p", [full("qk"), full("dg")], [("cn1", 0, 128)], lambda: te.matmul(T.cn1[:, 0:128], T.qk[:], T.dg[:], True, True))
-    V([full("idm")], [full("nid")], v1(T.nid[:], T.idm[:], -1.0, A.mult))
-    fill("cst2", 0, 128, 63.0 / 128.0)
-    V([], [full("cst2")], lambda: v.memset(T.cst2[0:1, :], 255.0))
-    c_ts(1)
-    c_ts(2)
-    V([full("bo"), full("cof")], [full("wto")], v1(T.wto[:], T.bo[:], T.cof[:, 4:5], A.mult))
-    V([("cn1", 0, 128)], [full("qm")], vc(T.qm[:], T.cn1[:, 0:128]))
-    for i in range(7):
-        before(0, i, (0,))
-    copy(col("o2f"), col("o2u"))
-    claim_rows(0, "o2f", 0, NL)
-    weave(claim_list(0))
-    S([("pl", 0, WW), full("vl")], [full("v0")], lambda: s.activation(T.v0[:], T.pl[:, 0:WW].indirect(T.vl[:, 0:12]), AF.Identity))
-    for i in range(8):
-        before(0, i, (1,) if i < 7 else (0, 1))
-    weave(scatter(0))
-    take("y", "m4", T.mo[:], [full("mo")])
-    sums(0)
-    for i in range(8):
-        rise(i)
-        if i < 6:
-            plain(i)
-    copy(col("mof", 0, 384), col(("mo", NL), 0, 384))
-    dma("y", T.yv[:, 0:NL], T.par0[0:128:16, :], [full("par0")], [])
-    for i in range(5):
-        before(1, i)
-    step1("dd", False, "mo", "mo", "o2u", "o2f", ("mo", NL), "mof", ("cof", 1), "q1", "t2u1", [nothing, nothing, lambda: scan(0)], 1)
-    shifted(1, "q1")
-    lots_of("q1")
-    stage("y1", T.tf, [full("tf")])
-    send("y1")
-    scan(1)
-    cl = claim_list(1)
-    weave(cl[:4])
-    scan(2)
-    weigh("wto")
-    weave(cl[4:])
-    before(1, 5)
-    weave(scatter(1), [nothing, nothing] + next_lots("q1", "tnu"))
-    before(1, 6)
-    before(1, 7)
-    sums(1)
-    for i in range(8):
-        rise(i)
-        if i < 6:
-            plain(i)
-    bound_sums()
-    bound_sel()
-    weave(pick("o2f", "mof", "b1f", 0), pick("pb1", ("mof", NL), "par12", NL))
-    copy(col("b1u"), col("b1f"))
-    take("y", "y1", T.yh[:, NL:2 * NL], [])
-    for i in range(5):
-        before(2, i)
-    step1("dd", False, "tnu", "tn", "t2u1", ("q1", ODD, 2), "b1u", "b1f", ("cof", 2), "q2", "t2u2", [nothing, nothing, nothing], 2)
-    lots_of("q2")
-    stage("y2", T.tf, [full("tf")])
-    send("y2")
-    bound_sums()
-    weave(claim_list(2))
-    before(2, 5)
-    weave(scatter(2), [nothing, bound_sel] + pick("pb2", "par12", ("par12", NL), 0))
-    before(2, 6)
-    before(2, 7)
-    stage("par", T.par12, [full("par12")], rows=True)
-    send("par")
-    sums(2)
-
-    def price(i):
-        lo, hi = 512 * i, 512 * i + 512
-        if i < 7:
-            S([("dd", lo, hi)], [("pf", lo, hi)], lambda: s.activation(T.pf[:, lo:hi], T.dd[:, lo:hi], AF.Identity, scale=-1.0, bias=MAGIC + 255.0))
+    def trial(t, tr, j):
+        r, n = R[t], CUTS[j + 1] - CUTS[j]
+        y, over, mk = items("ys%d" % tr, j), items("ind%d" % tr, j), "mk%d" % tr
+        theirs, ours = pick(r["tab"], lanes(r["a%du" % tr], j)), pick(r["tab"], lanes(r["tu"] if tr == 0 else "t1u", j))
+        if (t, tr, j) in APART:
+            first = 1024 * (len(apart) % 2)
+            apart.append(j)
+            act(col("yb", first, first + 16 * n), theirs)
+            act(col("xb", first, first + 16 * n), ours)
+            for h, db in enumerate(APART[(t, tr, j)]):
+                lo, hi = 8 * n * h, 8 * n * h + 8 * n
+                d = col(db, 0, 8 * n)
+                mm(d, [(c128("idm" if t == 0 else "nid"), col("xb", first + lo, first + hi)),
+                       (c128("nid" if t == 0 else "idm"), col("yb", first + lo, first + hi))])
+                act(col((over[1][0], over[1][1]), lo, hi), d, AF.Sign, bias=col(r["sg"], 0, 1))
         else:
-            V([("dd", lo, hi)], [("pf", lo, hi)], v2(T.pf[:, lo:hi], T.dd[:, lo:hi], -1.0, MAGIC + 255.0, A.mult, A.add))
+            for h in range(HALVES):
+                act(part(y, h), part(theirs, h), bias=col(r["sl"], 0, 1))
+                tt(part(over, h), part(ours, h), part(y, h), A.is_gt if t == 0 else A.is_lt)
+        cn = col(("cn%d" % (counted[0] % 2), 128 * (counted[0] // 2 % 4)), 0, n)
+        counted[0] += 1
+        mm(cn, [(c128("sel16", k), (col((over[1][0], over[1][1] + k, 16), 0, n)[0], over[1])) for k in range(16)])
+        src, out = (r["a0"], "tt") if tr == 0 else (r["a1"], r["q"])
+        new = lanes(odd(out), j)
+        tt(lanes(even(src), j), lanes(r["tn"] if tr == 0 else odd("tt"), j), lanes(odd(src), j), A.subtract)
+        ts(lanes(odd(mk), j), cn, 1.0 if (t, tr, j) in APART else 8.5, A.is_lt)
+        scan2(pairs(out, j), pairs(mk, j), pairs(src, j), A.add)
+        cp(lanes("t1u" if tr == 0 else r["t2u"] if t < 2 else "tf2", j), new)
 
-    def ship(b):
-        p, rp = col("pf", BLOCKS[b], BLOCKS[b + 1])
-        m = "o%d" % b
-        dma("y", T["s_" + m][:], p, [rp], [full("s_" + m)])
-        dma("y", T["l_" + m][rank], T.pf[mine, BLOCKS[b]:BLOCKS[b + 1]], [rp], [full("l_" + m)])
-        send(m)
-    nxt = 0
-    for i in range(8):
-        rise(i)
-        price(i)
-        if BLOCKS[nxt + 1] <= 512 * i + 512:
-            ship(nxt)
-            nxt += 1
-    take("s", "y2", T.yh[:, 2 * NL:3 * NL], [])
-    take("s", "par", T.yv[:, NL:3 * NL], [])
+    def next_lots(t, j):
+        r, z = R[t], lanes("m2", j)
+        for i in range(*j):
+            for h in range(HALVES):
+                act(part(items("x2", i), h), part(pick(r["tab"], lanes(r["t2u"], i)), h), **({} if t == 0 else {"scale": -1.0, "bias": 255.0}))
+            scan2(items("sc", i), col("rm", 0, 16 * (CUTS[i + 1] - CUTS[i])), items("x2", i), A.max)
+        mm(z, [(c128(r["wt"]), lanes(("sc", 15, 16), j))])
+        cp(lanes("ui", j), z)
+        ts(lanes("uj", j), lanes("ui", j), 2047, A.bitwise_and)
+        ts(z, lanes("uj", j), 33.0, A.add)
+        tt(lanes("pr", j), z, lanes(odd(r["q"]), j), A.mult)
+        ts(lanes("sm", j), lanes("pr", j), 2464.0 * (t + 1), A.add)
+        ts(lanes("tn", j), lanes("sm", j), 5, A.logical_shift_right, 4095, A.bitwise_and)
+        cp(lanes(r["nu"], j), lanes("tn", j))
+
+    def second_lots(t, j):
+        r, z = R[t], lanes(("m1", 300), j)
+        tt(lanes(even(r["a1"]), j), lanes(odd(r["a0"]), j), lanes(odd(r["a1"]), j), A.subtract)
+        mm(z, [(c128("nb"), lanes(odd("mk0"), j)), (c128("b17"), lanes(odd("mk1"), j))])
+        ts(lanes(odd("sp"), j), z, 256.5, A.is_ge)
+        scan2(pairs("bh", j), pairs("sp", j), pairs(r["a1"], j), A.add)
+        cp(lanes(r["bu"], j), lanes(odd("bh"), j))
+
+    def parent(t):
+        first, second, out = [c12(x) for x in R[t]["par"]]
+        stays = [c12(("m1", 272)), c12(("m1", 284) if t < 2 else "m2")]
+        terms = [[(c128("sel16", k), c12(odd("mk%d" % tr), k)) for k in range(16)] for tr in range(2)]
+        mm(stays[0], terms[0])
+        if t < 2:
+            mm(stays[1], terms[1])
+        else:
+            k = CUTS[-2] // 12
+            mm(stays[1], terms[1][:k], True, False)
+            mm(stays[1], terms[1][k:], False, True)
+        tt(c12("pd"), first, second, A.subtract)
+        ts(c12("hh"), stays[0], 15.0, A.max, 0.5, A.add)
+        tt(c12("ps"), stays[1], c12("hh"), A.is_gt)
+        tt(c12("pe"), c12("ps"), c12("pd"), A.mult)
+        tt(out, c12("pe"), second, A.add)
+
+    def step1(t):
+        for js in GROUPS:
+            for tr in range(2):
+                for j in range(*js):
+                    trial(t, tr, j)
+            if t < 2:
+                second_lots(t, js)
+                next_lots(t, js)
+        parent(t)
+
+    PLACES = {"a1u": (0, 1), "a0u": (2,), "tu": (3, 4)}
+
+    def claims(t):
+        tab, ml, cl, slack = ["ph", "c1", "c2"][t], "ml%d" % t, "cl%d" % t, [("csf", 0), ("cof", 5), ("cof", 6)][t]
+        act(col("ym", 0, 576), pick(tab, col(ml, 0, 36)), bias=col(slack, 0, 1))
+        tt(col("im", 0, 576), pick(tab, col(ml, 24, 60)), col("ym", 0, 576), A.is_gt if t == 0 else A.is_lt)
+        mm(col("m1", 0, 36), [(c128("sel16", k), (T.im[:, k:576:16], full("im"))) for k in range(16)])
+        ts(col("mf", 0, 48), col(ml, 0, 48), -2048.0, A.add)
+        tt(col("md", 0, 24), col("mf", 0, 24), col("mf", 24, 48), A.subtract)
+        ts(col("mm", 0, 36), col("m1", 0, 36), 8.5, A.is_ge)
+        ts(col("mm", 36, 48), col("m1", 24, 36), 8.5, A.is_lt)
+        tt(col("pq", 0, 24), col("mm", 0, 24), col("md", 0, 24), A.mult)
+        tt(col("pq2", 0, 24), col("pq", 0, 24), col("mf", 24, 48), A.add)
+        tt(col("prod", 0, 24), col("pq2", 0, 24), col("mm", 24, 48), A.mult)
+        tt(c12("lh"), c12("prod"), c12("prod", 1), A.add)
+        ts(col(cl, 24, 36), c12("lh"), 2048.0, A.add)
+        d, z = col(("m1", 64)), c12(("m1", 256))
+        mm([d] + [c12(("m1", 64), r) for r in range(16)],
+           [(col("eq", 0, 128, 16), col("tri", 0, NL, 16))] + [(c128("dm", r), c12("lh")) for r in range(16)])
+        ts(col("in2"), d, 0.0, A.is_equal, 8192.0, A.mult)
+        mm(z, [(c128("idh"), c12("lh"))] + [(c128("sel16", r), c12("in2", r)) for r in range(16)])
+        ts(c12(even(cl)), z, 2048.0, A.add, p3, A.min)
+
+    TAB = ["pl", "c1", "c2"]
+    CL = ["clo", "cl1", "cl2"]
+
+    def bank(t, i):
+        db, mode = cols(BANKS[int(DBS[t][i])], 0), RISE[t][i]
+        up = t == 2 and mode == "v"
+        k = 2 if t == 0 or up else 1
+        mm(db, [(col("cst3" if up else "cst2" if t == 0 else "cstb", 0, 128, k), col("oneb", 0, 512, k)),
+                (c128("nid" if t == 0 or up else "idm"), cols(TAB[t], i))], True, False)
+        mm(db, [(c128("qp" if up else "qm"), (cols("w%d" % t, i)[0], ("w%d" % t, 0, WW))),
+                (col("cstm", 0, 128, 1), col("oneb", 0, 512, 1))], False, True)
+        out = cols(TAB[t + 1] if t < 2 else "pf", i)
+        if mode == "v":
+            ts(out, db, -MAGIC, A.add, 0.0 if t < 2 else 255.0, A.max if t < 2 else A.min)
+        else:
+            act(out if t < 2 else cols("c1", i), db, AF.Relu, bias=-MAGIC)
+            if t == 2 and mode == "s":
+                ts(out, cols("c1", i), -1.0, A.mult, 255.0, A.add)
+            elif t == 2:
+                act(out, cols("c1", i), scale=-1.0, bias=255.0)
+
+    def step3(t):
+        act(col("vv"), pick(TAB[t], col(CL[t], 24, 36)), **({} if t == 0 else {"scale": -1.0, "bias": 255.0}))
+        for c in range(12):
+            cp(pick("w%d" % t, col(CL[t], 2 * c, 2 * c + 1), WW), col("vv", 16 * c, 16 * c + 16))
+        for i in range(8):
+            bank(t, i)
+
+    LISTS = (("ma", 512, 0, 8), ("mb", 256, 8, 12))
+
+    def lists_away(t, names):
+        cp(c12(("mb", NL)), c12("par%d" % t))
+        for m, (b, n, lo, hi) in zip(names, LISTS):
+            stage(m, T[b], 0, n, [full(b)])
+            send(m)
+            take(m, T[b + "o"][:], [full(b + "o")])
+
+    def lists_here(t):
+        for j in GROUPS:
+            cp(lanes(odd("qb"), j), lanes(R[t]["a0u"], j))
+            cp(lanes(odd("b1"), j), lanes(R[t]["a1u"], j))
+        cp(c12("pm%d" % t), c12(("mbo", NL)))
+
+    for b in range(len(FIRST) - 1):
+        send_wide("p%d" % b)
+        take("p%d" % b, T.pl[:, FIRST[b]:FIRST[b + 1]], [("pl", FIRST[b], FIRST[b + 1])])
+    send("cst")
+    take("cst", T.cso[:], [full("cso")])
+    cp(col("a0u"), col(("pk", 1344)))
+    cp(col("csf", 0, 3), col("cs", 0, 3))
+    ts(col("csf", 5, 6), col("cs", 0, 1), -1.0, A.mult, -0.5, A.add)
+    ts(col("csf", 6, 7), col("cs", 2, 3), -1.0, A.mult)
+    ts(col("csf", 7, 8), col("cs", 2, 3), -1.0, A.mult, -0.5, A.add)
+    cp(col("tu0"), col("lt"))
+    cp(c12(even("pvo")), c12("pvi"))
+    cp(c12("pvu"), c12("pvi"))
+    cp(col(odd("qa")), col(("pk", 1344)))
+    cp(col("ml0", 24, 48), col("mi", 0, 24))
+    cp(col("ml0", 48, 60), col("mi", 12, 24))
+    cp(col("csf", 4, 5), col("cs", 4, 5))
+    ts(c128("wth"), c128("bo"), col("csf", 4, 5), A.mult, 2.0, A.mult)
+    ts(col("a1h"), pick("pk", c12("pvu"), 1536), -2048.0, A.add, col("pcf", 5, 6), A.mult)
+    mm(c12("m1"), [(c128("sel16", k), (T.a1h[:, k:NL:16], full("a1h"))) for k in range(16)])
+    for k in range(2):
+        ts(c12("ml0", k), c12("m1"), 2048.0, A.add)
+    for c in range(12):
+        cp((T.b0[:, 2 * c + 1:384:24], ("b0", c, c + 1), 16), pick("pk", col("pvo", 2 * c, 2 * c + 1), 1536))
+    run("v", [full("b0")], [full("a1u"), full("b0")], NL * CYCLE, lambda: v.tensor_copy(T.a1u[:], T.b0[:, 1:384:2]))
+    claims(0)
+    stage("cl", T.cl0, 0, 40, [full("cl0")])
+    send("cl")
+    take("cl", T.clo[:], [full("clo")])
+    step1(0)
+    lists_away(0, ("ma", "mb"))
+    for m, n, lo, hi in LISTS:
+        for k in PLACES:
+            for pl in PLACES[k]:
+                o, first = col(("ml1", 12 * pl), lo, hi), 8 + 2 * R[1][k][2]
+                take(m, o[0], [o[1]], slice(first, first + 2))
+    for w in ("w1", "w2"):
+        zeros(w, [("order", 2, 3)])
+    act(col("tf0"), col(odd("q0")))
+    dma("y", T.yh[:, 0:NL], T.tf0[:], [full("tf0"), full("mbo")], [], 1e5)
+    dma("y", T.yv[:, 0:NL], c12("par0")[0], [full("par0"), full("mbo")], [], 1e4)
+    cp(col("cof", 0, 5), col("cso", 0, 5))
+    act(c128("dg"), c128("id64"), scale=col("cof", 3, 4))
+    mm(c128("db0"), [(c128("qk"), c128("dg"))])
+    act(c128("qm"), c128("db0"))
+    act(c128("qp"), c128("db0"), scale=-1.0)
+    act(col("cof", 5, 7), col("cof", 1, 3), scale=-1.0)
+    act(col("cof", 8, 9), col("cof", 1, 2), scale=-1.0, bias=-0.5)
+    act(col("cof", 7, 8), col("cof", 4, 5), scale=2.0)
+    act(c128("wto"), c128("bo"), scale=col("cof", 7, 8))
+    for k in range(4):
+        act(cols("selw", k), cols("sel16", k), scale=col("cof", 7, 8))
+    step3(0)
+    lists_here(1)
+    claims(1)
+    step3(1)
+    for b in range(len(FIRST) - 1):
+        lo, hi = FIRST[b], FIRST[b + 1]
+        stage("k%d" % b, T.c2, lo, hi, [("c2", lo, hi)])
+        send_wide("k%d" % b)
+        take("k%d" % b, T.ph[:, lo:hi], [("ph", lo, hi)])
+    step1(1)
+    z = c12(("m2", 256))
+    for j, (b, n, lo, hi) in zip(GROUPS, LISTS):
+        for k, x in (("a0u", "t2u"), ("a1u", "bu")):
+            x = lanes(R[1][x], j)[1]
+            for pl in PLACES[k]:
+                o = col(("ml2", 12 * pl), lo, hi)
+                dma("y", o[0], T[b][2:128:16, x[1]:x[2]], [x], [o[1]], 1e4)
+        n = hi - lo
+        mm(col(("m2", 256), lo, hi), [(c128("selw", k), col(("sc", 15, 16), CUTS[j[0]] + n * k, CUTS[j[0]] + n * k + n)) for k in range(16)])
+    cp(c12("si"), z)
+    ts(c12("si", 1), c12("si"), 2047, A.bitwise_and)
+    ts(z, c12("si", 1), 33.0, A.add)
+    tt(c12("si", 2), z, c12("ml2", 2), A.mult)
+    ts(c12("si", 3), c12("si", 2), 2464.0 * 2, A.add)
+    ts(c12("si"), c12("si", 3), 5, A.logical_shift_right, 4095, A.bitwise_and)
+    for pl in PLACES["tu"]:
+        cp(c12("ml2", pl), c12("si"))
+    lists_away(1, ("mc", "md"))
+    claims(2)
+    step3(2)
     for b in range(NB):
-        take("s", "o%d" % b, T.yp[:, BLOCKS[b]:BLOCKS[b + 1]], [])
+        stage("o%d" % b, T.pf, BLOCKS[b], BLOCKS[b + 1], [("pf", BLOCKS[b], BLOCKS[b + 1])])
+        send("o%d" % b)
+        take("o%d" % b, T.yp[:, BLOCKS[b]:BLOCKS[b + 1]], [])
+    lists_here(2)
+    act(col("tf1"), col(odd("qb")))
+    dma("s", T.yh[:, NL:2 * NL], T.tf1[:], [full("tf1")], [], 1e5)
+    dma("s", T.yv[:, NL:2 * NL], c12("pm2")[0], [full("pm2")], [], 1e4)
+    step1(2)
+    dma("s", T.yh[:, 2 * NL:3 * NL], T.tf2[:], [full("tf2")], [], 1e5)
+    dma("s", T.yv[:, 2 * NL:3 * NL], c12("par2")[0], [full("par2")], [], 1e4)
+    if not ORDER:
+        find_order()
+    for i in ORDER:
+        calls[i]["issue"]()
     for sem in sorted(total):
         if seen.get(sem, 0) < total[sem]:
             wait("g", sem, total[sem])

import numpy as np
from concourse.bass import DstId, RemoteDMATransfer
from concourse.mybir import dt, AluOpType, AxisListType, ActivationFunctionType

A = AluOpType
AF = ActivationFunctionType
MAGIC = 12582912.0
HALF = 63.0 / 128.0
NL = 192
E = 16 * NL
W = 4096
WW = W + 16
CUTS = [0, 64, 128, 192]
NC = len(CUTS) - 1
GROUPS = [(0, 2), (2, 3)]
HALVES = 2
BLOCKS = [0, 1024, 2048, 3072, W]
NB = len(BLOCKS) - 1
FIRST = [0, 2048, W]
RISE = ["svsvsvsv", "ssssssss", "svsvsvsv"]
DBS = ["45670123", "45673245", "45673245"]
APART = {}
CYCLE, PE_CYCLE, GATHER, SCATTER, WAKE = 1.0e-3, 0.5e-3, 1.6, 3.8, 0.1
DMA_BYTE, SEND_ISSUE, SEND_BYTE = 2.5e-6, 1.2, 0.8e-5
START = {"run": 0.0, "dma": 2.8, "send": 3.5}
EAGER = 10.0
PASSES = 8
SCRATCH = {}
PIECE = {}
ORDER = []
for _d, _n, _names in (
        ("bfloat16", W, "ph c1 c2 pf pl"), ("bfloat16", WW, "w0 w1 w2"), ("int32", 1536, "pk"),
        ("int32", NL, "lt ui uj pr sm tn"), ("int32", 12, "pvi"), ("int32", 24, "mi"), ("uint16", 24, "pvo"), ("uint16", 12, "pvu"),
        ("int32", 8, "cs cso pci"), ("float32", 8, "pcf"), ("float32", 10, "csf cof"), ("int32", 48, "si"), ("float32", 128, "cd cq cm"),
        ("float32", 384, "tt qa qb q0 q1 q2 b0 bh b1"), ("float32", 16, "lo hi"),
        ("bfloat16", 128, "bo nb b17 eq idm nid id64 qk dg qm qp wth wto cstb cstm cst2 cst3 zz z2"), ("bfloat16", 512, "oneb"),
        ("bfloat16", 2048, "sel16 selw xb yb"), ("float16", 2048, "dm"), ("float16", 128, "idh"), ("float16", 12, "lh"), ("float16", NL, "a1h"),
        ("bfloat16", E, "ind0 ind1 x2 sc"), ("bfloat16", 1536, "rm"), ("float32", E, "ys0 ys1"), ("bfloat16", NL, "vv tri in2"),
        ("bfloat16", 384, "mk0 mk1 sp"), ("float32", 576, "ym"), ("bfloat16", 576, "im"),
        ("float32", NL, "cm2 tf0 tf1 tf2"), ("uint16", 64, "ml0 ml1 ml2"), ("float32", 48, "mf mm"), ("float32", 24, "md pq pq2 prod"),
        ("uint16", 40, "cl0 cl1 cl2 clo"), ("float32", 12, "pbz pb0 pb1 pb2 hh pd ps pe par0 par1 par2 pm1 pm2"),
        ("uint16", NL, "tu0 a0u a1u t1u"), ("uint16", 512, "ma mao"), ("uint16", 256, "mb mbo")):
    _ks = _names.split()
    if (_d, _n) in (("bfloat16", 128), ("float32", 24), ("float32", 12)):
        SCRATCH["side%d" % _n] = ("sbuf", [128, _n * len(_ks)], _d)
        for _i, _k in enumerate(_ks):
            PIECE[_k] = ("side%d" % _n, _n * _i, _n * _i + _n)
    else:
        for _k in _ks:
            SCRATCH[_k] = ("sbuf", [128, _n], _d)
MSG = []
for _k, _n, _d in ([("cst", 1, "int32"), ("cl", 5, "uint16"), ("ma", 64, "uint16"), ("mb", 32, "uint16"), ("mc", 64, "uint16"), ("md", 32, "uint16")]
                   + [(_x + "%d" % _b, (FIRST[_b + 1] - FIRST[_b]) // 8, "bfloat16") for _b in range(len(FIRST) - 1) for _x in "pk"]
                   + [("o%d" % _b, (BLOCKS[_b + 1] - BLOCKS[_b]) // 8, "bfloat16") for _b in range(NB)]):
    MSG.append(_k)
    SCRATCH["s_" + _k] = SCRATCH["l_" + _k] = ("dram", [8, 128, _n], _d)
BANKS = ["cn0", "cn1", "m1", "m2", "db0", "db1", "db2", "db3"]
for _k in BANKS:
    SCRATCH[_k] = ("psum", [128, 512], "float32")
SEMAPHORES = ["vv", "ss", "pe", "gg", "lsem"] + ["d%d" % _i for _i in range(100)] + ["ar_" + _m for _m in MSG]
BYTES = {"bfloat16": 2, "float16": 2, "uint16": 2, "float32": 4, "int32": 4}


def rank_program(g, core, T, topo):
    rank = T.rank_of(core)
    if rank is None:
        return
    cores = [int(c) for c in T.cores]
    N = len(cores)

    eng = {"v": g.vector, "s": g.scalar, "p": g.tensor, "g": g, "y": g.sync}
    sem_of = {"v": "vv", "s": "ss", "p": "pe", "g": "gg"}
    count = {"vv": 0, "ss": 0, "pe": 0, "gg": 0, "d": 0}
    know = {q: {} for q in eng}
    snap = {}
    hist = {}
    total = {}
    seen = {}
    calls = []
    named = {}

    def wait(q, sem, val):
        if know[q].get(sem, 0) >= val:
            return
        eng[q].wait_ge(T.sem[sem], val)
        seen[sem] = max(seen.get(sem, 0), val)
        know[q][sem] = val
        for k, n in snap.get((sem, val), {}).items():
            know[q][k] = max(know[q].get(k, 0), n)

    def settle(q, reads, writes):
        for (b, lo, hi), wr in [(r, False) for r in reads] + [(w, True) for w in writes]:
            for e in hist.get(b, []):
                if (e[0] < hi and lo < e[1] and (wr or e[5])) or (b in BANKS and e[2] != q):
                    wait(q, e[3], e[4])

    def record(q, sem, val, reads, writes):
        for (b, lo, hi) in writes:
            hist[b] = [e for e in hist.get(b, []) if not (lo <= e[0] and e[1] <= hi)] + [(lo, hi, q, sem, val, True)]
        for (b, lo, hi) in reads:
            old = hist.get(b, [])
            hist[b] = [e for e in old if not (e[:3] == (lo, hi, q) and not e[5] and q != "d")] + [(lo, hi, q, sem, val, False)]

    def name(q, kind, reads, writes, busy, late, issue):
        me, after = len(calls), {}
        for (b, lo, hi), wr in [(r, False) for r in reads] + [(w, True) for w in writes]:
            for e in named.get(b, []):
                if e[0] < hi and lo < e[1] and (wr or e[3]):
                    after[e[2]] = after.get(e[2], False) or b != "order"
        for (b, lo, hi) in writes:
            named[b] = [e for e in named.get(b, []) if not (lo <= e[0] and e[1] <= hi)] + [(lo, hi, me, True)]
        for (b, lo, hi) in reads:
            named[b] = named.get(b, []) + [(lo, hi, me, False)]
        calls.append({"q": q, "kind": kind, "busy": busy, "late": late, "after": after, "issue": issue,
                      "banks": {x[0] for x in reads + writes if x[0] in BANKS}})

    def run(q, reads, writes, busy, *fns):
        def issue():
            settle(q, reads, writes)
            for f in fns[:-1]:
                f()
            sem = sem_of[q]
            count[sem] += 1
            val = total[sem] = count[sem]
            fns[-1]().then_inc(T.sem[sem], 1)
            snap[(sem, val)] = dict(know[q])
            snap[(sem, val)][sem] = val
            record(q, sem, val, reads, writes)
        name(q, "run", reads, writes, busy, 0.0, issue)

    def dma(q, out, in_, reads, writes, size, first=None, keep=False):
        def issue():
            if first is not None:
                first()
            settle(q, reads, writes)
            sem = "d%d" % count["d"]
            count["d"] += 1
            total[sem] = 16
            eng[q].dma_start(out, in_).then_inc(T.sem[sem], 16)
            snap[(sem, 16)] = dict(know[q])
            record("d", sem, 16, reads, writes)
        name(q, "dma", reads, writes + ([("order", "ys".index(q), "ys".index(q) + 1)] if keep else []), 0.06, size * DMA_BYTE, issue)

    def place(rank_of, after, lead, forward):
        n = len(calls)
        follow = [[] for c in calls]
        for i in range(n):
            for k in after[i]:
                follow[k].append(i)
        left = [len(a) for a in after]
        ready = {q: [i for i in range(n) if left[i] == 0 and calls[i]["q"] == q] for q in eng}
        free, line, lead = {q: 0.0 for q in eng}, {"dma": 0.0, "send": 0.0}, list(lead)
        order, done, used = [], [0.0] * n, {}

        def next_of(q):
            at = {i: max([free[q], lead[i]] + [used[b][1] + WAKE for b in calls[i]["banks"] if used.get(b, (q,))[0] != q]) for i in ready[q]}
            i = min(at, key=lambda k: (rank_of[k] + EAGER * at[k], k))
            return at[i], i
        for step in range(n):
            t, i = min(next_of(q) for q in eng if ready[q])
            c = calls[i]
            order.append(i)
            free[c["q"]] = done[i] = t + c["busy"]
            if forward and c["kind"] != "run":
                line[c["kind"]] = max(line[c["kind"]], done[i]) + c["late"]
                done[i] = line[c["kind"]] + START[c["kind"]]
            for b in c["banks"]:
                used[b] = (c["q"], done[i])
            ready[c["q"]].remove(i)
            for k in follow[i]:
                if after[k][i] is not None:
                    lead[k] = max(lead[k], done[i] + after[k][i])
                left[k] -= 1
                if left[k] == 0:
                    ready[calls[k]["q"]].append(k)
        return order, done

    def find_order():
        n = len(calls)
        late = [c["late"] + START[c["kind"]] for c in calls]
        ahead = [{k: WAKE if hard else None for k, hard in c["after"].items()} for c in calls]
        back = [{} for c in calls]
        for i in range(n):
            for k, hard in calls[i]["after"].items():
                back[k][i] = WAKE + late[k] if hard else None
        rank_of, best = [0.15 * i for i in range(n)], None
        for k in range(PASSES):
            order, done = place(rank_of, ahead, [0.0] * n, True)
            if best is None or max(done) < best[0]:
                best = (max(done), order)
            rank_of = [-t for t in place([-t for t in done], back, late, False)[1]]
        ORDER.extend(best[1])

    def full(b):
        return PIECE.get(b, (b, 0, 1 << 20))

    def col(x, lo=0, hi=NL, rows=128):
        if isinstance(x, str):
            x = (x, 0)
        (b, first), st = PIECE.get(x[0], (x[0], 0))[:2], x[2] if len(x) > 2 else 1
        i, j = first + x[1] + lo * st, first + x[1] + (hi - 1) * st + 1
        return (T[b][0:rows, i:j] if st == 1 else T[b][0:rows, i:j:st]), (b, i, j), hi - lo

    def pick(tab, lst, n=W):
        return (T[tab][:, 0:n].indirect(lst[0]), (tab, 0, n), 16 * lst[2], lst[1])

    v, s, te = g.vector, g.scalar, g.tensor

    def val(x):
        return x[0] if isinstance(x, tuple) else x

    def rd(o, *xs):
        return [x[1] for x in xs if isinstance(x, tuple)] + [x[3] for x in (o,) + xs if isinstance(x, tuple) and len(x) > 3]

    def width(x):
        return BYTES[SCRATCH[x[1][0]][2]]

    def lasts(o, a, *more, per=None):
        if len(o) > 3 or len(a) > 3:
            return 0.06 + o[2] * CYCLE * (SCATTER if len(o) > 3 else GATHER)
        return max(64, o[2] * (per or (0.5 if max(width(x) for x in (o, a) + more) == 2 else 1))) * CYCLE

    def tt(o, a, b, op):
        run("v", rd(o, a, b), [o[1]], lasts(o, a, per=1 if a[1][0] in BANKS or b[1][0] in BANKS else 2), lambda: v.tensor_tensor(o[0], a[0], b[0], op))

    def cp(o, a):
        run("v", rd(o, a), [o[1]], lasts(o, a), lambda: v.tensor_copy(o[0], a[0]))

    def ts(o, a, s1, op0, s2=None, op1=None):
        if op1 is None:
            run("v", rd(o, a, s1), [o[1]], lasts(o, a), lambda: v.tensor_scalar(o[0], a[0], val(s1), None, op0))
        else:
            run("v", rd(o, a, s1, s2), [o[1]], lasts(o, a), lambda: v.tensor_scalar(o[0], a[0], val(s1), val(s2), op0, op1))

    def scan2(o, d0, d1, op1):
        run("v", rd(o, d0, d1), [o[1]], lasts(o, d0, d1), lambda: v.tensor_tensor_scan(o[0], d0[0], d1[0], 0.0, A.mult, op1))

    def act(o, a, f=AF.Identity, **kw):
        run("s", rd(o, a, *kw.values()), [o[1]], 0.06 + lasts(o, a, per=1), lambda: s.activation(o[0], a[0], f, **{k: val(x) for k, x in kw.items()}))

    def fill(b, lo, hi, x, rows=128):
        o = col(b, lo, hi, rows)
        run("v", [], [o[1]], lasts(o, o), lambda: v.memset(o[0], x))

    def mm(out, terms, start=True, stop=True):
        outs = out if isinstance(out, list) else [out] * len(terms)
        last = len(terms) - 1
        run("p", [x[1] for t in terms for x in t], [o[1] for o in outs], sum(max(64, o[2]) for o in outs) * PE_CYCLE,
            *[(lambda k=k: te.matmul(outs[k][0], terms[k][0][0], terms[k][1][0], start and k == 0, stop and k == last)) for k in range(last + 1)])

    def c128(b, k=0):
        return col(b, 128 * k, 128 * k + 128)

    def c12(b, k=0):
        return col(b, 12 * k, 12 * k + 12)

    def cols(b, i):
        return col(b, 512 * i, 512 * i + 512)

    def odd(b):
        return (b, 1, 2)

    def even(b):
        return (b, 0, 2)

    others = [(rank + j) % N for j in range(1, N)]
    away = [d for d in others if topo.chip(cores[d]) != topo.chip(core)]
    near = [d for d in others if topo.chip(cores[d]) == topo.chip(core)]
    offe = topo.engines(core, cores[away[0]])
    one = [e for e in topo.engines(core, cores[near[0]]) if e not in offe]
    turn = [0]
    arrive = {m: 0 for m in MSG}

    def size_of(m):
        return 8 * 128 * SCRATCH["s_" + m][1][2] * BYTES[SCRATCH["s_" + m][2]]

    def fused(m, plan, part):
        def issue():
            settle("g", [full("s_" + m)], [])
            tr, n = [], 0
            for d, es in plan():
                rid, pid, _e = topo.addr(cores[d])
                tr.append(RemoteDMATransfer(dst_ids=[DstId(rid=rid, pnc=pid)], dma_engine_mask=sum(1 << e for e in es),
                                            remote_sem=T.sem["ar_" + m], src=T["s_" + m][d], dst=T["l_" + m][rank]))
                n += len(es)
            g.remote_dma_fused(tr, local_sem=T.sem.lsem)
            total["lsem"] = total.get("lsem", 0) + n
            arrive[m] += n
        name("g", "send", [full("s_" + m)], [("ar_" + m, part[0], part[0] + 1), ("order", 2, 3)], SEND_ISSUE, size_of(m) * SEND_BYTE / part[1], issue)

    def send(m):
        def plan():
            turn[0] += len(away)
            return [(d, [offe[(turn[0] + j) % len(offe)]]) for j, d in enumerate(away)] + [(d, one[0:3:2]) for d in near]
        fused(m, plan, (0, 1))

    def send_wide(m):
        fused(m, lambda: [(d, offe[2 * j:2 * j + 2]) for j, d in enumerate(away[:4])] + [(d, one[0:3:2]) for d in near], (0, 2))
        fused(m, lambda: [(d, offe[4 * j:4 * j + 4]) for j, d in enumerate(away[4:])], (1, 2))

    def landed(q, m):
        total["ar_" + m] = arrive[m]
        wait(q, "ar_" + m, arrive[m])

    mine = slice(16 * rank, 16 * rank + 16)

    def stage(m, src, lo, hi, reads, keep=False):
        dma("y", T["s_" + m][:], src[:, lo:hi], reads, [full("s_" + m)], size_of(m), keep=keep)
        dma("y", T["l_" + m][rank], src[mine, lo:hi], reads, [full("l_" + m)], size_of(m) // 8, keep=keep)

    def take(m, out, writes, rows=slice(0, 128)):
        dma("y", out, T["l_" + m][:, rows, :], [full("l_" + m), full("ar_" + m)], writes, size_of(m) * (rows.stop - rows.start) // 128,
            lambda: landed("y", m))

    def load(q, o, src, size=1e5):
        dma(q, o[0], src, [], [o[1]], size, keep=True)
    load("y", col("lt"), T.lots[:])
    load("s", col("pk", 1344, 1536), T.packs[:, 1344:1536])
    load("y", col("cs", 0, 3), T.slack[:])
    load("s", c12("pvi"), T.prev[:, 1344:1536])
    load("y", col("ph", 0, W), T.price[:], 1e6)
    fill("cs", 4, 8, 0)
    load("s", c12("mi"), T.packs[0:128:16, 1344:1536])
    load("s", c12("mi", 1), T.lots[0:128:16, :])
    load("s", col("cs", 3, 4), T.inc[:])
    dma("s", T.cs[:, 4:5], T.wt[:], [], [("cs", 4, 8)], 1e5, keep=True)
    stage("p0", T.price, FIRST[0], FIRST[1], [], keep=True)
    load("y", col("pk", 0, 1344), T.packs[:, 0:1344], 7e5)
    for b in range(1, len(FIRST) - 1):
        stage("p%d" % b, T.price, FIRST[b], FIRST[b + 1], [], keep=True)
    stage("cst", T.cs, 0, 8, [full("cs")])

    def iota(b, lo, hi, pat, more=()):
        o = col(b, lo, hi)
        run("g", list(more), [o[1]], 0.13 + 2 * o[2] * CYCLE, lambda: g.iota(o[0], pat, 0, 0, allow_small_or_imprecise_dtypes=True))

    def zeros(w, more=()):
        for k in range(8):
            iota(w, WW * k // 8, WW * (k + 1) // 8, [[0, WW // 8]], more)
    run("g", [], [("pci", 0, 1)], 0.13, lambda: g.iota(T.pci[:, 0:1], [[0, 1]], 0, 1))
    iota("cd", 0, 128, [[1, 8], [0, 16]])
    iota("cq", 0, 128, [[1, 128]])
    iota("cm2", 0, NL, [[1, 16], [0, 12]])
    iota("pbz", 0, 12, [[1, 12]])
    iota("cm", 0, 128, [[0, 8], [1, 16]])
    for k in ("mk0", "mk1", "sp"):
        iota(k, 0, 384, [[0, 384]])
    zeros("w0")
    p0, p1, p2, p3 = [col("pcf", k, k + 1) for k in range(4)]
    fill("sel16", 0, 2048, 0.0)
    ts(col("pci", 1, 2), col("pci", 0, 1), 15, A.bitwise_and)
    ts(col("pci", 2, 3), col("pci", 0, 1), 4, A.logical_shift_right)
    widest = max(CUTS[j + 1] - CUTS[j] for j in range(NC))
    fill("rm", 0, 16 * widest, 1.0)
    fill(("rm", 0, 16), 0, widest, 0.0)
    cp(col("pcf", 0, 3), col("pci", 0, 3))
    ts(c128("bo"), c128("cd"), p2, A.is_equal)
    ts(c128("z2"), c128("cq"), p0, A.is_equal, 2.0, A.mult)
    ts(col("lo", 0, 16), col("cq", 0, 16), p1, A.is_equal, -1.0, A.mult)
    ts(col("hi", 0, 16), col("cq", 0, 16), p1, A.not_equal)
    for k in range(16):
        act(col(("sel16", 129 * k, 16), 0, 8), col(("bo", 0, 16), 0, 8), AF.Copy)
    tt(c128("zz"), c128("z2"), c128("bo"), A.subtract)
    ts(c128("idm"), c128("cq"), p0, A.is_equal)
    ts(c128("idh"), c128("cq"), p0, A.is_equal)
    for r in range(16):
        ts(c128("dm", r), c128("zz"), col("lo", r, r + 1), A.max, col("hi", r, r + 1), A.min)
    ts(col("tri"), col("cm2"), p1, A.is_le, 8192.0, A.mult)
    ts(p3, p1, float(W), A.add)
    ts(col("pcf", 4, 5), p1, 12.0, A.mult, 1344.0, A.add)
    ts(col("pcf", 5, 6), p1, 0.0, A.is_equal)
    ts(c128("nb"), c128("bo"), -1.0, A.mult)
    ts(c128("b17"), c128("bo"), 17.0, A.mult)
    ts(c128("eq"), c128("cm"), p1, A.is_equal)
    for t in range(3):
        ts(c12("pb%d" % t), c12("pbz"), col("pcf", 4, 5), A.add, float(NL * t), A.add)
        fill("cl%d" % t, 0, 40, 0)
    fill("ma", 384, 512, 0)
    fill("mb", NL, 256, 0)
    tt(c128("qk"), c128("eq"), c128("idm"), A.subtract)
    ts(c128("nid"), c128("idm"), -1.0, A.mult)
    ts(c128("id64"), c128("idm"), -1.0 / 64.0, A.mult)
    fill("cstb", 0, 128, HALF)
    fill("cstm", 0, 128, MAGIC)
    fill("cst2", 0, 128, HALF)
    fill("cst3", 0, 128, -HALF)
    fill("oneb", 0, 512, 1.0)
    for k in ("cst2", "cst3"):
        fill(k, 0, 128, 255.0, 1)

    def lanes(x, j):
        j, k = j if isinstance(j, tuple) else (j, j + 1)
        if isinstance(x, list):
            x = (x[0], CUTS[-2] * x[2]) if j < NC - 1 else (x[1], (NL - CUTS[-2]) * x[2] - CUTS[-2])
        return col(x, CUTS[j], CUTS[k])

    def items(b, j):
        return col(b, 16 * CUTS[j], 16 * CUTS[j + 1])

    def pairs(b, j):
        j, k = j if isinstance(j, tuple) else (j, j + 1)
        return col(b, 2 * CUTS[j], 2 * CUTS[k])

    came = dict(a0u=["mao", "mbo", 0], a1u=["mao", "mbo", 1], tu=["mao", "mbo", 2], tn=["mao", "mbo", 2], a0="qb", a1="b1")
    goes = dict(t2u=["ma", "mb", 0], bu=["ma", "mb", 1], nu=["ma", "mb", 2])
    R = [dict(tab="ph", tu="tu0", tn="lt", a0u="a0u", a0="qa", a1u="a1u", a1="b0", sl=("csf", 0), sg=("csf", 5), q="q0", wt="wth",
              par=("pb0", "pvi", "par0"), **goes),
         dict(tab="c1", sl=("cof", 5), sg=("cof", 8), q="q1", wt="wto", par=("pb1", "pm1", "par1"), **came, **goes),
         dict(tab="ph", sl=("csf", 6), sg=("csf", 7), q="q2", par=("pb2", "pm2", "par2"), **came)]
    counted, apart = [0], []

    def part(x, h):
        b, lo, hi = x[-1] if len(x) > 3 else x[1]
        n = (hi - lo) // HALVES
        y = col(b, lo + n * h, lo + n * h + n)
        return pick(x[1][0], y) if len(x) > 3 else y

    def trial(t, tr, j):
        r, n = R[t], CUTS[j + 1] - CUTS[j]
        y, over, mk = items("ys%d" % tr, j), items("ind%d" % tr, j), "mk%d" % tr
        theirs, ours = pick(r["tab"], lanes(r["a%du" % tr], j)), pick(r["tab"], lanes(r["tu"] if tr == 0 else "t1u", j))
        if (t, tr, j) in APART:
            first = 1024 * (len(apart) % 2)
            apart.append(j)
            act(col("yb", first, first + 16 * n), theirs)
            act(col("xb", first, first + 16 * n), ours)
            for h, db in enumerate(APART[(t, tr, j)]):
                lo, hi = 8 * n * h, 8 * n * h + 8 * n
                d = col(db, 0, 8 * n)
                mm(d, [(c128("idm" if t == 0 else "nid"), col("xb", first + lo, first + hi)),
                       (c128("nid" if t == 0 else "idm"), col("yb", first + lo, first + hi))])
                act(col((over[1][0], over[1][1]), lo, hi), d, AF.Sign, bias=col(r["sg"], 0, 1))
        else:
            for h in range(HALVES):
                act(part(y, h), part(theirs, h), bias=col(r["sl"], 0, 1))
                tt(part(over, h), part(ours, h), part(y, h), A.is_gt if t == 0 else A.is_lt)
        cn = col(("cn%d" % (counted[0] % 2), 128 * (counted[0] // 2 % 4)), 0, n)
        counted[0] += 1
        mm(cn, [(c128("sel16", k), (col((over[1][0], over[1][1] + k, 16), 0, n)[0], over[1])) for k in range(16)])
        src, out = (r["a0"], "tt") if tr == 0 else (r["a1"], r["q"])
        new = lanes(odd(out), j)
        tt(lanes(even(src), j), lanes(r["tn"] if tr == 0 else odd("tt"), j), lanes(odd(src), j), A.subtract)
        ts(lanes(odd(mk), j), cn, 1.0 if (t, tr, j) in APART else 8.5, A.is_lt)
        scan2(pairs(out, j), pairs(mk, j), pairs(src, j), A.add)
        cp(lanes("t1u" if tr == 0 else r["t2u"] if t < 2 else "tf2", j), new)

    def next_lots(t, j):
        r, z = R[t], lanes("m2", j)
        for i in range(*j):
            for h in range(HALVES):
                act(part(items("x2", i), h), part(pick(r["tab"], lanes(r["t2u"], i)), h), **({} if t == 0 else {"scale": -1.0, "bias": 255.0}))
            scan2(items("sc", i), col("rm", 0, 16 * (CUTS[i + 1] - CUTS[i])), items("x2", i), A.max)
        mm(z, [(c128(r["wt"]), lanes(("sc", 15, 16), j))])
        cp(lanes("ui", j), z)
        ts(lanes("uj", j), lanes("ui", j), 2047, A.bitwise_and)
        ts(z, lanes("uj", j), 33.0, A.add)
        tt(lanes("pr", j), z, lanes(odd(r["q"]), j), A.mult)
        ts(lanes("sm", j), lanes("pr", j), 2464.0 * (t + 1), A.add)
        ts(lanes("tn", j), lanes("sm", j), 5, A.logical_shift_right, 4095, A.bitwise_and)
        cp(lanes(r["nu"], j), lanes("tn", j))

    def second_lots(t, j):
        r, z = R[t], lanes(("m1", 300), j)
        tt(lanes(even(r["a1"]), j), lanes(odd(r["a0"]), j), lanes(odd(r["a1"]), j), A.subtract)
        mm(z, [(c128("nb"), lanes(odd("mk0"), j)), (c128("b17"), lanes(odd("mk1"), j))])
        ts(lanes(odd("sp"), j), z, 256.5, A.is_ge)
        scan2(pairs("bh", j), pairs("sp", j), pairs(r["a1"], j), A.add)
        cp(lanes(r["bu"], j), lanes(odd("bh"), j))

    def parent(t):
        first, second, out = [c12(x) for x in R[t]["par"]]
        stays = [c12(("m1", 272)), c12(("m1", 284) if t < 2 else "m2")]
        terms = [[(c128("sel16", k), c12(odd("mk%d" % tr), k)) for k in range(16)] for tr in range(2)]
        mm(stays[0], terms[0])
        if t < 2:
            mm(stays[1], terms[1])
        else:
            k = CUTS[-2] // 12
            mm(stays[1], terms[1][:k], True, False)
            mm(stays[1], terms[1][k:], False, True)
        tt(c12("pd"), first, second, A.subtract)
        ts(c12("hh"), stays[0], 15.0, A.max, 0.5, A.add)
        tt(c12("ps"), stays[1], c12("hh"), A.is_gt)
        tt(c12("pe"), c12("ps"), c12("pd"), A.mult)
        tt(out, c12("pe"), second, A.add)

    def step1(t):
        for js in GROUPS:
            for tr in range(2):
                for j in range(*js):
                    trial(t, tr, j)
            if t < 2:
                second_lots(t, js)
                next_lots(t, js)
        parent(t)

    PLACES = {"a1u": (0, 1), "a0u": (2,), "tu": (3, 4)}

    def claims(t):
        tab, ml, cl, slack = ["ph", "c1", "c2"][t], "ml%d" % t, "cl%d" % t, [("csf", 0), ("cof", 5), ("cof", 6)][t]
        act(col("ym", 0, 576), pick(tab, col(ml, 0, 36)), bias=col(slack, 0, 1))
        tt(col("im", 0, 576), pick(tab, col(ml, 24, 60)), col("ym", 0, 576), A.is_gt if t == 0 else A.is_lt)
        mm(col("m1", 0, 36), [(c128("sel16", k), (T.im[:, k:576:16], full("im"))) for k in range(16)])
        ts(col("mf", 0, 48), col(ml, 0, 48), -2048.0, A.add)
        tt(col("md", 0, 24), col("mf", 0, 24), col("mf", 24, 48), A.subtract)
        ts(col("mm", 0, 36), col("m1", 0, 36), 8.5, A.is_ge)
        ts(col("mm", 36, 48), col("m1", 24, 36), 8.5, A.is_lt)
        tt(col("pq", 0, 24), col("mm", 0, 24), col("md", 0, 24), A.mult)
        tt(col("pq2", 0, 24), col("pq", 0, 24), col("mf", 24, 48), A.add)
        tt(col("prod", 0, 24), col("pq2", 0, 24), col("mm", 24, 48), A.mult)
        tt(c12("lh"), c12("prod"), c12("prod", 1), A.add)
        ts(col(cl, 24, 36), c12("lh"), 2048.0, A.add)
        d, z = col(("m1", 64)), c12(("m1", 256))
        mm([d] + [c12(("m1", 64), r) for r in range(16)],
           [(col("eq", 0, 128, 16), col("tri", 0, NL, 16))] + [(c128("dm", r), c12("lh")) for r in range(16)])
        ts(col("in2"), d, 0.0, A.is_equal, 8192.0, A.mult)
        mm(z, [(c128("idh"), c12("lh"))] + [(c128("sel16", r), c12("in2", r)) for r in range(16)])
        ts(c12(even(cl)), z, 2048.0, A.add, p3, A.min)

    TAB = ["pl", "c1", "c2"]
    CL = ["clo", "cl1", "cl2"]

    def bank(t, i):
        db, mode = cols(BANKS[int(DBS[t][i])], 0), RISE[t][i]
        up = t == 2 and mode == "v"
        k = 2 if t == 0 or up else 1
        mm(db, [(col("cst3" if up else "cst2" if t == 0 else "cstb", 0, 128, k), col("oneb", 0, 512, k)),
                (c128("nid" if t == 0 or up else "idm"), cols(TAB[t], i))], True, False)
        mm(db, [(c128("qp" if up else "qm"), (cols("w%d" % t, i)[0], ("w%d" % t, 0, WW))),
                (col("cstm", 0, 128, 1), col("oneb", 0, 512, 1))], False, True)
        out = cols(TAB[t + 1] if t < 2 else "pf", i)
        if mode == "v":
            ts(out, db, -MAGIC, A.add, 0.0 if t < 2 else 255.0, A.max if t < 2 else A.min)
        else:
            act(out if t < 2 else cols("c1", i), db, AF.Relu, bias=-MAGIC)
            if t == 2 and mode == "s":
                ts(out, cols("c1", i), -1.0, A.mult, 255.0, A.add)
            elif t == 2:
                act(out, cols("c1", i), scale=-1.0, bias=255.0)

    def step3(t):
        act(col("vv"), pick(TAB[t], col(CL[t], 24, 36)), **({} if t == 0 else {"scale": -1.0, "bias": 255.0}))
        for c in range(12):
            cp(pick("w%d" % t, col(CL[t], 2 * c, 2 * c + 1), WW), col("vv", 16 * c, 16 * c + 16))
        for i in range(8):
            bank(t, i)

    LISTS = (("ma", 512, 0, 8), ("mb", 256, 8, 12))

    def lists_away(t, names):
        cp(c12(("mb", NL)), c12("par%d" % t))
        for m, (b, n, lo, hi) in zip(names, LISTS):
            stage(m, T[b], 0, n, [full(b)])
            send(m)
            take(m, T[b + "o"][:], [full(b + "o")])

    def lists_here(t):
        for j in GROUPS:
            cp(lanes(odd("qb"), j), lanes(R[t]["a0u"], j))
            cp(lanes(odd("b1"), j), lanes(R[t]["a1u"], j))
        cp(c12("pm%d" % t), c12(("mbo", NL)))

    for b in range(len(FIRST) - 1):
        send_wide("p%d" % b)
        take("p%d" % b, T.pl[:, FIRST[b]:FIRST[b + 1]], [("pl", FIRST[b], FIRST[b + 1])])
    send("cst")
    take("cst", T.cso[:], [full("cso")])
    cp(col("a0u"), col(("pk", 1344)))
    cp(col("csf", 0, 3), col("cs", 0, 3))
    ts(col("csf", 5, 6), col("cs", 0, 1), -1.0, A.mult, -0.5, A.add)
    ts(col("csf", 6, 7), col("cs", 2, 3), -1.0, A.mult)
    ts(col("csf", 7, 8), col("cs", 2, 3), -1.0, A.mult, -0.5, A.add)
    cp(col("tu0"), col("lt"))
    cp(c12(even("pvo")), c12("pvi"))
    cp(c12("pvu"), c12("pvi"))
    cp(col(odd("qa")), col(("pk", 1344)))
    cp(col("ml0", 24, 48), col("mi", 0, 24))
    cp(col("ml0", 48, 60), col("mi", 12, 24))
    cp(col("csf", 4, 5), col("cs", 4, 5))
    ts(c128("wth"), c128("bo"), col("csf", 4, 5), A.mult, 2.0, A.mult)
    ts(col("a1h"), pick("pk", c12("pvu"), 1536), -2048.0, A.add, col("pcf", 5, 6), A.mult)
    mm(c12("m1"), [(c128("sel16", k), (T.a1h[:, k:NL:16], full("a1h"))) for k in range(16)])
    for k in range(2):
        ts(c12("ml0", k), c12("m1"), 2048.0, A.add)
    for c in range(12):
        cp((T.b0[:, 2 * c + 1:384:24], ("b0", c, c + 1), 16), pick("pk", col("pvo", 2 * c, 2 * c + 1), 1536))
    run("v", [full("b0")], [full("a1u"), full("b0")], NL * CYCLE, lambda: v.tensor_copy(T.a1u[:], T.b0[:, 1:384:2]))
    claims(0)
    stage("cl", T.cl0, 0, 40, [full("cl0")])
    send("cl")
    take("cl", T.clo[:], [full("clo")])
    step1(0)
    lists_away(0, ("ma", "mb"))
    for m, n, lo, hi in LISTS:
        for k in PLACES:
            for pl in PLACES[k]:
                o, first = col(("ml1", 12 * pl), lo, hi), 8 + 2 * R[1][k][2]
                take(m, o[0], [o[1]], slice(first, first + 2))
    for w in ("w1", "w2"):
        zeros(w, [("order", 2, 3)])
    act(col("tf0"), col(odd("q0")))
    dma("y", T.yh[:, 0:NL], T.tf0[:], [full("tf0"), full("mbo")], [], 1e5)
    dma("y", T.yv[:, 0:NL], c12("par0")[0], [full("par0"), full("mbo")], [], 1e4)
    cp(col("cof", 0, 5), col("cso", 0, 5))
    act(c128("dg"), c128("id64"), scale=col("cof", 3, 4))
    mm(c128("db0"), [(c128("qk"), c128("dg"))])
    act(c128("qm"), c128("db0"))
    act(c128("qp"), c128("db0"), scale=-1.0)
    act(col("cof", 5, 7), col("cof", 1, 3), scale=-1.0)
    act(col("cof", 8, 9), col("cof", 1, 2), scale=-1.0, bias=-0.5)
    act(col("cof", 7, 8), col("cof", 4, 5), scale=2.0)
    act(c128("wto"), c128("bo"), scale=col("cof", 7, 8))
    for k in range(4):
        act(cols("selw", k), cols("sel16", k), scale=col("cof", 7, 8))
    step3(0)
    lists_here(1)
    claims(1)
    step3(1)
    for b in range(len(FIRST) - 1):
        lo, hi = FIRST[b], FIRST[b + 1]
        stage("k%d" % b, T.c2, lo, hi, [("c2", lo, hi)])
        send_wide("k%d" % b)
        take("k%d" % b, T.ph[:, lo:hi], [("ph", lo, hi)])
    step1(1)
    z = c12(("m2", 256))
    for j, (b, n, lo, hi) in zip(GROUPS, LISTS):
        for k, x in (("a0u", "t2u"), ("a1u", "bu")):
            x = lanes(R[1][x], j)[1]
            for pl in PLACES[k]:
                o = col(("ml2", 12 * pl), lo, hi)
                dma("y", o[0], T[b][2:128:16, x[1]:x[2]], [x], [o[1]], 1e4)
        n = hi - lo
        mm(col(("m2", 256), lo, hi), [(c128("selw", k), col(("sc", 15, 16), CUTS[j[0]] + n * k, CUTS[j[0]] + n * k + n)) for k in range(16)])
    cp(c12("si"), z)
    ts(c12("si", 1), c12("si"), 2047, A.bitwise_and)
    ts(z, c12("si", 1), 33.0, A.add)
    tt(c12("si", 2), z, c12("ml2", 2), A.mult)
    ts(c12("si", 3), c12("si", 2), 2464.0 * 2, A.add)
    ts(c12("si"), c12("si", 3), 5, A.logical_shift_right, 4095, A.bitwise_and)
    for pl in PLACES["tu"]:
        cp(c12("ml2", pl), c12("si"))
    lists_away(1, ("mc", "md"))
    claims(2)
    step3(2)
    for b in range(NB):
        stage("o%d" % b, T.pf, BLOCKS[b], BLOCKS[b + 1], [("pf", BLOCKS[b], BLOCKS[b + 1])])
        send("o%d" % b)
        take("o%d" % b, T.yp[:, BLOCKS[b]:BLOCKS[b + 1]], [])
    lists_here(2)
    act(col("tf1"), col(odd("qb")))
    dma("s", T.yh[:, NL:2 * NL], T.tf1[:], [full("tf1")], [], 1e5)
    dma("s", T.yv[:, NL:2 * NL], c12("pm2")[0], [full("pm2")], [], 1e4)
    step1(2)
    dma("s", T.yh[:, 2 * NL:3 * NL], T.tf2[:], [full("tf2")], [], 1e5)
    dma("s", T.yv[:, 2 * NL:3 * NL], c12("par2")[0], [full("par2")], [], 1e4)
    if not ORDER:
        find_order()
    for i in ORDER:
        calls[i]["issue"]()
    for sem in sorted(total):
        if seen.get(sem, 0) < total[sem]:
            wait("g", sem, total[sem])
